import numpy as np
import ml_dtypes


def mxq(x, axis, fmt="e4m3"):
    dtype, down = {"e4m3": (ml_dtypes.float8_e4m3fn, 7), "e5m2": (ml_dtypes.float8_e5m2, 14)}[fmt]
    v = np.moveaxis(np.asarray(x, np.float32).astype(ml_dtypes.bfloat16).astype(np.float64), axis, -1)
    blocks = v.reshape(v.shape[:-1] + (-1, 32))
    amax = np.abs(blocks).max(-1, keepdims=True)
    byte = np.maximum(np.where(amax > 0, np.frexp(amax)[1] - 1 + 127, 0) - down, 1)
    scale = np.exp2(byte - 127.0)
    codes = (blocks / scale).astype(np.float32).astype(dtype).astype(np.float64)
    return np.moveaxis((codes * scale).reshape(v.shape), -1, axis)


WIDE = False


def mx_kscale(k):
    if not WIDE:
        return np.ones(k)
    levels = np.array([10, -10, 5, -5, 0])
    if k % 512:
        return np.exp2(np.random.permutation(np.resize(levels, k // 32))).repeat(32)
    a = np.empty((k // 512, 16))
    for p in range(k // 512):
        a[p, :8] = np.random.permutation(np.resize(levels, 8))
        for g in range(8):
            far = levels[np.abs(levels - a[p, g]) >= 10]
            a[p, g + 8] = far[np.random.randint(len(far))]
    return np.exp2(a.ravel()).repeat(32)


def f64(x):
    return np.asarray(x).astype(np.float64)


def striped(idx):
    return np.tile(np.asarray(idx).reshape(-1, 16).T, (8, 1)).astype(np.uint16)


def unstriped(offs):
    return offs[:16].T.reshape(-1).astype(np.int64)


E2M1 = np.array([0.0, 0.5, 1.0, 1.5, 2.0, 3.0, 4.0, 6.0, -0.0, -0.5, -1.0, -1.5, -2.0, -3.0, -4.0, -6.0])


def pack_weight(w, fmt):
    k, n = w.shape
    w = f64(np.asarray(w, np.float32).astype(ml_dtypes.bfloat16)).reshape(k // 32, 32, n)
    amax = np.abs(w).max(1)
    if fmt == "e4m3":
        byte = np.frexp(amax)[1] - 1 + 127 - 7
    else:
        mant, ex = np.frexp(amax / 6.0)
        byte = np.where(mant > 0.5, ex, ex - 1) + 127
    byte = np.clip(np.where(amax > 0, byte, 1), 1, 254)
    scaled = (w * np.exp2(127.0 - byte)[:, None, :]).reshape(k, n).astype(np.float32)
    by_word = np.ascontiguousarray(scaled.reshape(k // 512, 128, 4, n).transpose(0, 1, 3, 2))
    if fmt == "e4m3":
        words = by_word.astype(ml_dtypes.float8_e4m3fn).view(np.uint8)
    else:
        c = by_word.astype(ml_dtypes.float4_e2m1fn).view(np.uint8) & 0xF
        words = (c[..., 0::2] | (c[..., 1::2] << 4)).reshape(k // 512, 128, 2 * n)
    return np.ascontiguousarray(words), np.ascontiguousarray(byte.astype(np.uint8).reshape(k // 512, 16, n))


def unpack_weight(words, scales, fmt):
    g, _, n = scales.shape
    words = np.ascontiguousarray(words).reshape(g, 128, n, -1)
    if fmt == "e4m3":
        vals = words.view(ml_dtypes.float8_e4m3fn).astype(np.float64)
    else:
        nib = np.empty((g, 128, n, 4), np.uint8)
        nib[..., 0::2] = words & 0xF
        nib[..., 1::2] = words >> 4
        vals = E2M1[nib]
    vals = vals * np.repeat(np.exp2(scales.astype(np.float64) - 127.0), 8, axis=1)[..., None]
    return vals.transpose(0, 1, 3, 2).reshape(g * 512, n)


def bf(x):
    return np.asarray(x, np.float32).astype(ml_dtypes.bfloat16)


def planes(Y):
    r, m = Y.shape
    b = f64(bf(Y)).reshape(r // 32, 32, m)
    amax = np.abs(b).max(1)
    byte = np.clip(np.where(amax > 0, np.frexp(amax)[1] - 1 + 127 - 7, 1), 1, 254)
    codes = (b * np.exp2(127.0 - byte)[:, None, :]).reshape(r, m).astype(np.float32).astype(ml_dtypes.float8_e4m3fn).view(np.uint8)
    words = codes.reshape(r // 512, 128, 4, m).transpose(0, 1, 3, 2)
    return np.ascontiguousarray(words), np.ascontiguousarray(byte.astype(np.uint8).reshape(r // 512, 16, m))


K, T, R, U, I, F, M = 512, 2048, 512, 2048, 512, 512, 512


def setup_inputs():
    n = np.random.standard_normal
    idx = np.random.permutation(T)[:I]
    idx2 = np.random.permutation(U)[:I]
    fk = mx_kscale(K)
    fr = mx_kscale(R)
    ff = mx_kscale(F)
    quesp = pack_weight(n((K, T)) / fk[:, None], "e4m3")
    imgp = pack_weight(n((R, U)) / fr[:, None], "e4m3")
    return {
        "ques_words": quesp[0],
        "ques_scales": quesp[1],
        "img_words": imgp[0],
        "img_scales": imgp[1],
        "wq": (n((K, F)) * 1 / np.sqrt(K) * fk[:, None]).astype(np.float32),
        "wi": (n((R, F)) * 1 / np.sqrt(R) * fr[:, None]).astype(np.float32),
        "gain": (np.random.uniform(0.5, 2.0, (F, 1)) * ff[:, None]).astype(np.float32),
        "wo": (n((F, M)) * 2 / np.sqrt(F) / ff[:, None]).astype(np.float32),
        "offs": striped(idx),
        "offs2": striped(idx2),
    }


def reference(ques_words, ques_scales, img_words, img_scales, wq, wi, gain, wo, offs, offs2):
    idx = unstriped(offs)
    idx2 = unstriped(offs2)
    quesu = unpack_weight(ques_words, ques_scales, "e4m3")
    imgu = unpack_weight(img_words, img_scales, "e4m3")
    wqq = mxq(f64(wq), 0, "e4m3")
    quesidxg = quesu[:, idx]
    z = wqq.T @ quesidxg
    wiq = mxq(f64(wi), 0, "e4m3")
    imgidx2g = imgu[:, idx2]
    v = wiq.T @ imgidx2g
    x = np.tanh(z) * np.tanh(v) * f64(gain)
    woq = mxq(f64(wo), 0, "e4m3")
    xq = mxq(x, 0, "e4m3")
    y = woq.T @ xq
    words, scales = planes(y)
    return y, words, scales

@@ -1,0 +1,199 @@
+from contextlib import ExitStack
+
+import concourse.mybir as mybir
+
+F32 = mybir.dt.float32
+BF16 = mybir.dt.bfloat16
+I32 = mybir.dt.int32
+U32 = mybir.dt.uint32
+U16 = mybir.dt.uint16
+U8 = mybir.dt.uint8
+FP8X4 = mybir.dt.float8_e4m3fn_x4
+TANH = mybir.ActivationFunctionType.Tanh
+MULT = mybir.AluOpType.mult
+
+P = 128
+PACK = 4
+WIDTH = 512
+TABLE = 2048
+HALF = 256
+QUARTER = 128
+IMG_SCALE_ROW = 4
+WQ_SPLIT = 40
+COPY = mybir.ActivationFunctionType.Copy
+
+FLOPS = 3 * 2 * 512 * 512 * 512
+
+
+def tile_attend_bilinearfuse_pl_kernel(
+    tc, ques_words, ques_scales, img_words, img_scales, wq, wi, gain, wo, offs, offs2, out_0, out_1, out_2
+):
+    nc = tc.nc
+    with ExitStack() as ctx:
+        keep = ctx.enter_context(tc.tile_pool(name="keep", bufs=1))
+        psum = ctx.enter_context(tc.psum_pool(name="psum", bufs=4))
+
+        def new(shape, dtype, name, tag=None):
+            return keep.tile(shape, dtype, name=name, tag=tag or name, align_bytes=64)
+
+        offs_t = keep.tile([P, WIDTH // 16], U16, name="offs_t")
+        offs2_t = keep.tile([P, WIDTH // 16], U16, name="offs2_t")
+        gain_t = new([P, PACK], F32, "gain_t")
+        q_words = new([P, TABLE], U32, "q_words")
+        i_words = new([P, TABLE], U32, "i_words")
+        q_scales = new([P, TABLE], U8, "q_scales")
+        i_scales = new([P, TABLE], U8, "i_scales")
+        raw = {n: new([P, PACK, WIDTH], F32, n + "_raw") for n in ("wq", "wi")}
+        wo_raw = [new([P, PACK, HALF], F32, f"wo_raw{h}") for h in range(2)]
+        dealt = {n: new([P, PACK * WIDTH], BF16, n + "_bf") for n in ("wq", "wi", "wo")}
+        codes = {n: new([P, WIDTH], U32, n + "_codes") for n in ("wi", "wo")}
+        scales = {n: new([P, WIDTH], U8, n + "_scales") for n in ("wq", "wi", "wo")}
+
+        def load_weight(n, w):
+            nc.sync.dma_start(raw[n][:], w.rearrange("(p j) c -> p j c", j=PACK))
+
+        def load_words(tile, words):
+            nc.sync.dma_start(tile[:].bitcast(I32), words[0].rearrange("p n t -> p (n t)").bitcast(I32))
+
+        def load_scales(queue, tile, rows, first):
+            for quad in range(4):
+                lo = 32 * quad + first
+                queue.dma_start(tile[lo : lo + 4, :].bitcast(I32), rows[0, 4 * quad : 4 * quad + 4, :].bitcast(I32))
+
+        nc.vector.memset(q_scales[:].bitcast(I32), 0)
+        nc.vector.memset(i_scales[:].bitcast(I32), 0)
+        load_weight("wq", wq)
+        nc.sync.dma_start(offs_t[:], offs)
+        nc.sync.dma_start(offs2_t[:], offs2)
+        load_scales(nc.sync, q_scales, ques_scales, 0)
+        load_words(q_words, ques_words)
+        load_scales(nc.sync, i_scales, img_scales, IMG_SCALE_ROW)
+        load_weight("wi", wi)
+        nc.sync.dma_start(gain_t[:], gain.rearrange("(p t) o -> p (t o)", t=PACK))
+        wo_rows = wo.rearrange("(p j) c -> p j c", j=PACK)
+        nc.sync.dma_start(wo_raw[0][:], wo_rows[:, :, 0:HALF])
+        load_words(i_words, img_words)
+        nc.sync.dma_start(wo_raw[1][:], wo_rows[:, :, HALF:WIDTH])
+
+        def deal_wo(copy, h, lo, hi):
+            dst = dealt["wo"][:].rearrange("p (t m j) -> p m j t", t=PACK, j=PACK)
+            src = wo_raw[h][:].rearrange("p j (m t) -> p m j t", t=PACK)
+            copy(dst[:, 64 * h + lo : 64 * h + hi], src[:, lo:hi])
+
+        def deal(copy, n, lo, hi):
+            src = raw[n][:].rearrange("p j (m t) -> p m j t", t=PACK)
+            dst = dealt[n][:].rearrange("p (t m j) -> p m j t", t=PACK, j=PACK)
+            copy(dst[:, lo:hi], src[:, lo:hi])
+
+        def quantise_weight(n):
+            nc.vector.quantize_mx(codes[n][:].bitcast(FP8X4), scales[n][:], dealt[n][:])
+
+        def product(out, n, t, rhs, rhs_scale):
+            cols = slice(t * P, (t + 1) * P)
+            nc.tensor.matmul_mx(
+                out,
+                lhsT=codes[n][:, cols].bitcast(FP8X4),
+                lhsT_scale=scales[n][:, cols],
+                rhs=rhs.bitcast(FP8X4),
+                rhs_scale=rhs_scale,
+                start=True,
+                stop=True,
+            )
+
+        q_picked = new([P, WIDTH], U32, "q_picked")
+        q_picked_scales = new([P, WIDTH], U8, "q_picked_scales")
+        i_picked = new([P, WIDTH], U32, "i_picked")
+        i_picked_scales = new([P, WIDTH], U8, "i_picked_scales")
+
+        deal(nc.vector.tensor_copy, "wq", 0, WQ_SPLIT)
+        deal(nc.scalar.copy, "wq", WQ_SPLIT, P)
+        nc.vector.tensor_copy(q_picked_scales[:], q_scales[:].indirect(offs_t[:]))
+        codes["wq"] = new([P, WIDTH], U32, "wq_codes", "q_scales")
+        quantise_weight("wq")
+
+        tanh_z = [new([P, 2, WIDTH], F32, f"tanh_z{u}") for u in range(2)]
+        for h in range(2):
+            cols = slice(h * HALF, (h + 1) * HALF)
+            nc.vector.tensor_copy(q_picked[:, cols], q_words[:].indirect(offs_t[:, 16 * h : 16 * h + 16]))
+            for u in range(2):
+                bank = psum.tile([P, 2, HALF], F32, name="zy")
+                for e in range(2):
+                    product(bank[:, e, :], "wq", 2 * u + e, q_picked[:, cols], q_picked_scales[:, cols])
+                nc.scalar.activation(tanh_z[u][:, :, cols], bank[:], TANH)
+        nc.vector.tensor_copy(i_picked_scales[:], i_scales[:].indirect(offs2_t[:]))
+        deal(nc.vector.tensor_copy, "wi", 0, P)
+        quantise_weight("wi")
+
+        gained = new([P, WIDTH // 4, PACK, 4], F32, "gained")
+        for t in range(PACK):
+            nc.scalar.activation(
+                gained[:, :, t, :],
+                tanh_z[t // 2][:, t % 2, :].rearrange("p (c i) -> p c i", i=4),
+                COPY,
+                scale=gain_t[:, t : t + 1],
+            )
+        deal_wo(nc.vector.tensor_copy, 0, 0, 64)
+
+        x_codes = new([P, WIDTH], U32, "x_codes")
+        x_scales = new([P, WIDTH], U8, "x_scales")
+        y_codes = new([P, WIDTH], U32, "y_codes")
+        y_scales = new([P, WIDTH], U8, "y_scales")
+        out_rows = out_0.rearrange("(p t) i -> p t i", t=PACK)
+        out_words = out_1[0].rearrange("p n t -> p (n t)").bitcast(I32)
+
+        for h in range(2):
+            cols = slice(h * HALF, (h + 1) * HALF)
+            nc.vector.tensor_copy(i_picked[:, cols], i_words[:].indirect(offs2_t[:, 16 * h : 16 * h + 16]))
+        deal_wo(nc.vector.tensor_copy, 1, 0, 32)
+        deal_wo(nc.scalar.copy, 1, 32, 64)
+        quantise_weight("wo")
+
+        tanh_v = new([P, WIDTH // 4, PACK, 4], F32, "tanh_v", "wo_raw1")
+        x_bf = new([P, PACK * WIDTH], BF16, "x_bf", "wo_bf")
+        for q in range(4):
+            cols = slice(q * QUARTER, (q + 1) * QUARTER)
+            bank = psum.tile([P, PACK, QUARTER], F32, name="v")
+            for t in range(PACK):
+                product(bank[:, t, :], "wi", t, i_picked[:, cols], i_picked_scales[IMG_SCALE_ROW:P, cols])
+            nc.scalar.activation(
+                tanh_v[:, 32 * q : 32 * q + 32], bank[:].rearrange("p t (c i) -> p c t i", i=4), TANH
+            )
+
+        y_banks = []
+        for q in range(4):
+            cols = slice(q * QUARTER, (q + 1) * QUARTER)
+            xb = x_bf[:, PACK * q * QUARTER : PACK * (q + 1) * QUARTER]
+            nc.vector.tensor_tensor(
+                xb.rearrange("p (c i t) -> p c t i", i=4, t=PACK),
+                gained[:, 32 * q : 32 * q + 32],
+                tanh_v[:, 32 * q : 32 * q + 32],
+                MULT,
+            )
+            nc.vector.quantize_mx(x_codes[:, cols].bitcast(FP8X4), x_scales[:, cols], xb)
+            bank = psum.tile([P, PACK, QUARTER], F32, name="zy")
+            for t in range(PACK):
+                product(bank[:, t, :], "wo", t, x_codes[:, cols], x_scales[:, cols])
+            y_banks.append(bank)
+
+        for q in range(4):
+            cols = slice(q * QUARTER, (q + 1) * QUARTER)
+            y = new([P, PACK, QUARTER], F32, f"y{q}")
+            yb = new([P, PACK * QUARTER], BF16, f"y_bf{q}")
+            if q == 3:
+                nc.scalar.copy(yb[:].rearrange("p (i t) -> p i t", t=PACK), y_banks[q][:].rearrange("p t i -> p i t"))
+            nc.scalar.copy(y[:], y_banks[q][:])
+            nc.sync.dma_start(out_rows[:, :, cols], y[:])
+            if q < 3:
+                nc.vector.tensor_copy(
+                    yb[:].rearrange("p (c i t) -> p c t i", i=4, t=PACK),
+                    y[:].rearrange("p t (c i) -> p c t i", i=4),
+                )
+            nc.vector.quantize_mx(y_codes[:, cols].bitcast(FP8X4), y_scales[:, cols], yb[:])
+            if q % 2 == 1:
+                half = slice((q - 1) * QUARTER, (q + 1) * QUARTER)
+                nc.sync.dma_start(out_words[:, half], y_codes[:, half].bitcast(I32))
+        for quad in range(4):
+            queue = nc.scalar if quad % 2 else nc.sync
+            queue.dma_start(
+                out_2[0, 4 * quad : 4 * quad + 4, :].bitcast(I32), y_scales[32 * quad : 32 * quad + 4, :].bitcast(I32)
+            )

@@ -44,7 +44,7 @@ def tile_attend_bilinearfuse_pl_kernel(
         q_scales = new([P, TABLE], U8, "q_scales")
         i_scales = new([P, TABLE], U8, "i_scales")
         raw = {n: new([P, PACK, WIDTH], F32, n + "_raw") for n in ("wq", "wi")}
-        wo_raw = [new([P, PACK, HALF], F32, f"wo_raw{h}") for h in range(2)]
+        wo_raw = [new([P, 2, WIDTH], F32, f"wo_raw{h}") for h in range(2)]
         dealt = {n: new([P, PACK * WIDTH], BF16, n + "_bf") for n in ("wq", "wi", "wo")}
         codes = {n: new([P, WIDTH], U32, n + "_codes") for n in ("wi", "wo")}
         scales = {n: new([P, WIDTH], U8, n + "_scales") for n in ("wq", "wi", "wo")}
@@ -56,29 +56,28 @@ def tile_attend_bilinearfuse_pl_kernel(
             nc.sync.dma_start(tile[:].bitcast(I32), words[0].rearrange("p n t -> p (n t)").bitcast(I32))
 
         def load_scales(queue, tile, rows, first):
-            for quad in range(4):
-                lo = 32 * quad + first
-                queue.dma_start(tile[lo : lo + 4, :].bitcast(I32), rows[0, 4 * quad : 4 * quad + 4, :].bitcast(I32))
+            for r in range(4):
+                queue.dma_start(tile[first + r : P : 32, :].bitcast(I32), rows[0, r:16:4, :].bitcast(I32))
 
         nc.vector.memset(q_scales[:].bitcast(I32), 0)
-        nc.vector.memset(i_scales[:].bitcast(I32), 0)
+        nc.gpsimd.memset(i_scales[:].bitcast(I32), 0)
         load_weight("wq", wq)
         nc.sync.dma_start(offs_t[:], offs)
         nc.sync.dma_start(offs2_t[:], offs2)
         load_scales(nc.sync, q_scales, ques_scales, 0)
         load_words(q_words, ques_words)
-        load_scales(nc.sync, i_scales, img_scales, IMG_SCALE_ROW)
+        load_scales(nc.gpsimd, i_scales, img_scales, IMG_SCALE_ROW)
         load_weight("wi", wi)
         nc.sync.dma_start(gain_t[:], gain.rearrange("(p t) o -> p (t o)", t=PACK))
         wo_rows = wo.rearrange("(p j) c -> p j c", j=PACK)
-        nc.sync.dma_start(wo_raw[0][:], wo_rows[:, :, 0:HALF])
         load_words(i_words, img_words)
-        nc.sync.dma_start(wo_raw[1][:], wo_rows[:, :, HALF:WIDTH])
+        for h in range(2):
+            nc.sync.dma_start(wo_raw[h][:], wo_rows[:, 2 * h : 2 * h + 2, :])
 
-        def deal_wo(copy, h, lo, hi):
+        def deal_wo(h):
             dst = dealt["wo"][:].rearrange("p (t m j) -> p m j t", t=PACK, j=PACK)
             src = wo_raw[h][:].rearrange("p j (m t) -> p m j t", t=PACK)
-            copy(dst[:, 64 * h + lo : 64 * h + hi], src[:, lo:hi])
+            nc.vector.tensor_copy(dst[:, :, 2 * h : 2 * h + 2, :], src)
 
         def deal(copy, n, lo, hi):
             src = raw[n][:].rearrange("p j (m t) -> p m j t", t=PACK)
@@ -103,7 +102,6 @@ def tile_attend_bilinearfuse_pl_kernel(
         q_picked = new([P, WIDTH], U32, "q_picked")
         q_picked_scales = new([P, WIDTH], U8, "q_picked_scales")
         i_picked = new([P, WIDTH], U32, "i_picked")
-        i_picked_scales = new([P, WIDTH], U8, "i_picked_scales")
 
         deal(nc.vector.tensor_copy, "wq", 0, WQ_SPLIT)
         deal(nc.scalar.copy, "wq", WQ_SPLIT, P)
@@ -120,6 +118,7 @@ def tile_attend_bilinearfuse_pl_kernel(
                 for e in range(2):
                     product(bank[:, e, :], "wq", 2 * u + e, q_picked[:, cols], q_picked_scales[:, cols])
                 nc.scalar.activation(tanh_z[u][:, :, cols], bank[:], TANH)
+        i_picked_scales = new([P, WIDTH], U8, "i_picked_scales", "q_words")
         nc.vector.tensor_copy(i_picked_scales[:], i_scales[:].indirect(offs2_t[:]))
         deal(nc.vector.tensor_copy, "wi", 0, P)
         quantise_weight("wi")
@@ -132,7 +131,6 @@ def tile_attend_bilinearfuse_pl_kernel(
                 COPY,
                 scale=gain_t[:, t : t + 1],
             )
-        deal_wo(nc.vector.tensor_copy, 0, 0, 64)
 
         x_codes = new([P, WIDTH], U32, "x_codes")
         x_scales = new([P, WIDTH], U8, "x_scales")
@@ -144,12 +142,11 @@ def tile_attend_bilinearfuse_pl_kernel(
         for h in range(2):
             cols = slice(h * HALF, (h + 1) * HALF)
             nc.vector.tensor_copy(i_picked[:, cols], i_words[:].indirect(offs2_t[:, 16 * h : 16 * h + 16]))
-        deal_wo(nc.vector.tensor_copy, 1, 0, 32)
-        deal_wo(nc.scalar.copy, 1, 32, 64)
-        quantise_weight("wo")
+        for h in range(2):
+            deal_wo(h)
 
-        tanh_v = new([P, WIDTH // 4, PACK, 4], F32, "tanh_v", "wo_raw1")
-        x_bf = new([P, PACK * WIDTH], BF16, "x_bf", "wo_bf")
+        tanh_v = new([P, WIDTH // 4, PACK, 4], F32, "tanh_v")
+        x_bf = new([P, PACK * WIDTH], BF16, "x_bf", "wo_raw1")
         for q in range(4):
             cols = slice(q * QUARTER, (q + 1) * QUARTER)
             bank = psum.tile([P, PACK, QUARTER], F32, name="v")
@@ -169,31 +166,38 @@ def tile_attend_bilinearfuse_pl_kernel(
                 tanh_v[:, 32 * q : 32 * q + 32],
                 MULT,
             )
+            if q == 0:
+                quantise_weight("wo")
             nc.vector.quantize_mx(x_codes[:, cols].bitcast(FP8X4), x_scales[:, cols], xb)
             bank = psum.tile([P, PACK, QUARTER], F32, name="zy")
             for t in range(PACK):
                 product(bank[:, t, :], "wo", t, x_codes[:, cols], x_scales[:, cols])
             y_banks.append(bank)
 
+        y_bf = new([P, PACK * WIDTH], BF16, "y_bf")
+
+        def quantise_y(lo, hi):
+            nc.vector.quantize_mx(
+                y_codes[:, lo:hi].bitcast(FP8X4), y_scales[:, lo:hi], y_bf[:, PACK * lo : PACK * hi]
+            )
+
         for q in range(4):
             cols = slice(q * QUARTER, (q + 1) * QUARTER)
             y = new([P, PACK, QUARTER], F32, f"y{q}")
-            yb = new([P, PACK * QUARTER], BF16, f"y_bf{q}")
-            if q == 3:
-                nc.scalar.copy(yb[:].rearrange("p (i t) -> p i t", t=PACK), y_banks[q][:].rearrange("p t i -> p i t"))
+            yb = y_bf[:, PACK * q * QUARTER : PACK * (q + 1) * QUARTER]
             nc.scalar.copy(y[:], y_banks[q][:])
             nc.sync.dma_start(out_rows[:, :, cols], y[:])
-            if q < 3:
+            if q == 0:
+                nc.scalar.copy(yb.rearrange("p (i t) -> p i t", t=PACK), y_banks[q][:].rearrange("p t i -> p i t"))
+            else:
                 nc.vector.tensor_copy(
-                    yb[:].rearrange("p (c i t) -> p c t i", i=4, t=PACK),
+                    yb.rearrange("p (c i t) -> p c t i", i=4, t=PACK),
                     y[:].rearrange("p t (c i) -> p c t i", i=4),
                 )
-            nc.vector.quantize_mx(y_codes[:, cols].bitcast(FP8X4), y_scales[:, cols], yb[:])
-            if q % 2 == 1:
-                half = slice((q - 1) * QUARTER, (q + 1) * QUARTER)
-                nc.sync.dma_start(out_words[:, half], y_codes[:, half].bitcast(I32))
-        for quad in range(4):
-            queue = nc.scalar if quad % 2 else nc.sync
-            queue.dma_start(
-                out_2[0, 4 * quad : 4 * quad + 4, :].bitcast(I32), y_scales[32 * quad : 32 * quad + 4, :].bitcast(I32)
-            )
+                quantise_y(0 if q == 1 else q * QUARTER, (q + 1) * QUARTER)
+            if q >= 2:
+                done = slice(0 if q == 2 else q * QUARTER, (q + 1) * QUARTER)
+                nc.sync.dma_start(out_words[:, done], y_codes[:, done].bitcast(I32))
+        for r in range(4):
+            queue = nc.sync if r % 2 else nc.scalar
+            queue.dma_start(out_2[0, r:16:4, :].bitcast(I32), y_scales[r:P:32, :].bitcast(I32))

@@ -20,6 +20,7 @@ HALF = 256
 QUARTER = 128
 IMG_SCALE_ROW = 4
 WQ_SPLIT = 40
+WO_SPLIT = 96
 COPY = mybir.ActivationFunctionType.Copy
 
 FLOPS = 3 * 2 * 512 * 512 * 512
@@ -31,6 +32,7 @@ def tile_attend_bilinearfuse_pl_kernel(
     nc = tc.nc
     with ExitStack() as ctx:
         keep = ctx.enter_context(tc.tile_pool(name="keep", bufs=1))
+        late = ctx.enter_context(tc.tile_pool(name="late", bufs=1))
         psum = ctx.enter_context(tc.psum_pool(name="psum", bufs=4))
 
         def new(shape, dtype, name, tag=None):
@@ -44,7 +46,7 @@ def tile_attend_bilinearfuse_pl_kernel(
         q_scales = new([P, TABLE], U8, "q_scales")
         i_scales = new([P, TABLE], U8, "i_scales")
         raw = {n: new([P, PACK, WIDTH], F32, n + "_raw") for n in ("wq", "wi")}
-        wo_raw = [new([P, 2, WIDTH], F32, f"wo_raw{h}") for h in range(2)]
+        raw["wo"] = late.tile([P, PACK, WIDTH], F32, name="wo_raw", align_bytes=64, offset=0)
         dealt = {n: new([P, PACK * WIDTH], BF16, n + "_bf") for n in ("wq", "wi", "wo")}
         codes = {n: new([P, WIDTH], U32, n + "_codes") for n in ("wi", "wo")}
         scales = {n: new([P, WIDTH], U8, n + "_scales") for n in ("wq", "wi", "wo")}
@@ -60,24 +62,17 @@ def tile_attend_bilinearfuse_pl_kernel(
                 queue.dma_start(tile[first + r : P : 32, :].bitcast(I32), rows[0, r:16:4, :].bitcast(I32))
 
         nc.vector.memset(q_scales[:].bitcast(I32), 0)
-        nc.gpsimd.memset(i_scales[:].bitcast(I32), 0)
+        nc.vector.memset(i_scales[:].bitcast(I32), 0)
         load_weight("wq", wq)
         nc.sync.dma_start(offs_t[:], offs)
         nc.sync.dma_start(offs2_t[:], offs2)
         load_scales(nc.sync, q_scales, ques_scales, 0)
         load_words(q_words, ques_words)
-        load_scales(nc.gpsimd, i_scales, img_scales, IMG_SCALE_ROW)
+        load_scales(nc.sync, i_scales, img_scales, IMG_SCALE_ROW)
         load_weight("wi", wi)
-        nc.sync.dma_start(gain_t[:], gain.rearrange("(p t) o -> p (t o)", t=PACK))
-        wo_rows = wo.rearrange("(p j) c -> p j c", j=PACK)
         load_words(i_words, img_words)
-        for h in range(2):
-            nc.sync.dma_start(wo_raw[h][:], wo_rows[:, 2 * h : 2 * h + 2, :])
-
-        def deal_wo(h):
-            dst = dealt["wo"][:].rearrange("p (t m j) -> p m j t", t=PACK, j=PACK)
-            src = wo_raw[h][:].rearrange("p j (m t) -> p m j t", t=PACK)
-            nc.vector.tensor_copy(dst[:, :, 2 * h : 2 * h + 2, :], src)
+        nc.sync.dma_start(gain_t[:], gain.rearrange("(p t) o -> p (t o)", t=PACK))
+        load_weight("wo", wo)
 
         def deal(copy, n, lo, hi):
             src = raw[n][:].rearrange("p j (m t) -> p m j t", t=PACK)
@@ -102,6 +97,7 @@ def tile_attend_bilinearfuse_pl_kernel(
         q_picked = new([P, WIDTH], U32, "q_picked")
         q_picked_scales = new([P, WIDTH], U8, "q_picked_scales")
         i_picked = new([P, WIDTH], U32, "i_picked")
+        i_picked_scales = new([P, WIDTH], U8, "i_picked_scales")
 
         deal(nc.vector.tensor_copy, "wq", 0, WQ_SPLIT)
         deal(nc.scalar.copy, "wq", WQ_SPLIT, P)
@@ -118,19 +114,17 @@ def tile_attend_bilinearfuse_pl_kernel(
                 for e in range(2):
                     product(bank[:, e, :], "wq", 2 * u + e, q_picked[:, cols], q_picked_scales[:, cols])
                 nc.scalar.activation(tanh_z[u][:, :, cols], bank[:], TANH)
-        i_picked_scales = new([P, WIDTH], U8, "i_picked_scales", "q_words")
         nc.vector.tensor_copy(i_picked_scales[:], i_scales[:].indirect(offs2_t[:]))
         deal(nc.vector.tensor_copy, "wi", 0, P)
         quantise_weight("wi")
 
         gained = new([P, WIDTH // 4, PACK, 4], F32, "gained")
         for t in range(PACK):
-            nc.scalar.activation(
-                gained[:, :, t, :],
-                tanh_z[t // 2][:, t % 2, :].rearrange("p (c i) -> p c i", i=4),
-                COPY,
-                scale=gain_t[:, t : t + 1],
-            )
+            plain = tanh_z[t // 2][:, t % 2, :].rearrange("p (c i) -> p c i", i=4)
+            if t == PACK - 1:
+                nc.vector.tensor_scalar_mul(gained[:, :, t, :], plain, gain_t[:, t : t + 1])
+            else:
+                nc.scalar.activation(gained[:, :, t, :], plain, COPY, scale=gain_t[:, t : t + 1])
 
         x_codes = new([P, WIDTH], U32, "x_codes")
         x_scales = new([P, WIDTH], U8, "x_scales")
@@ -142,28 +136,32 @@ def tile_attend_bilinearfuse_pl_kernel(
         for h in range(2):
             cols = slice(h * HALF, (h + 1) * HALF)
             nc.vector.tensor_copy(i_picked[:, cols], i_words[:].indirect(offs2_t[:, 16 * h : 16 * h + 16]))
-        for h in range(2):
-            deal_wo(h)
+        deal(nc.vector.tensor_copy, "wo", 0, WO_SPLIT)
+        deal(nc.scalar.copy, "wo", WO_SPLIT, P)
 
-        tanh_v = new([P, WIDTH // 4, PACK, 4], F32, "tanh_v")
-        x_bf = new([P, PACK * WIDTH], BF16, "x_bf", "wo_raw1")
+        tanh_v_first = new([P, 32, PACK, 4], F32, "tanh_v_first")
+        tanh_v_rest = late.tile([P, 96, PACK, 4], F32, name="tanh_v_rest", align_bytes=64, offset=0)
+        tanh_v = [tanh_v_first[:]] + [tanh_v_rest[:, 32 * q : 32 * q + 32] for q in range(3)]
+        x_first = late.tile([P, PACK * QUARTER], BF16, name="x_first", align_bytes=64, offset=6144)
+        x_rest = new([P, 3 * PACK * QUARTER], BF16, "x_rest")
+        x_bf = [x_first[:]] + [x_rest[:, 512 * q : 512 * q + 512] for q in range(3)]
         for q in range(4):
             cols = slice(q * QUARTER, (q + 1) * QUARTER)
-            bank = psum.tile([P, PACK, QUARTER], F32, name="v")
+            bank = psum.tile([P, PACK, QUARTER], F32, name="v", bufs=2)
             for t in range(PACK):
                 product(bank[:, t, :], "wi", t, i_picked[:, cols], i_picked_scales[IMG_SCALE_ROW:P, cols])
             nc.scalar.activation(
-                tanh_v[:, 32 * q : 32 * q + 32], bank[:].rearrange("p t (c i) -> p c t i", i=4), TANH
+                tanh_v[q], bank[:].rearrange("p t (c i) -> p c t i", i=4), TANH
             )
 
         y_banks = []
         for q in range(4):
             cols = slice(q * QUARTER, (q + 1) * QUARTER)
-            xb = x_bf[:, PACK * q * QUARTER : PACK * (q + 1) * QUARTER]
+            xb = x_bf[q]
             nc.vector.tensor_tensor(
                 xb.rearrange("p (c i t) -> p c t i", i=4, t=PACK),
                 gained[:, 32 * q : 32 * q + 32],
-                tanh_v[:, 32 * q : 32 * q + 32],
+                tanh_v[q],
                 MULT,
             )
             if q == 0:
@@ -195,9 +193,7 @@ def tile_attend_bilinearfuse_pl_kernel(
                     y[:].rearrange("p t (c i) -> p c t i", i=4),
                 )
                 quantise_y(0 if q == 1 else q * QUARTER, (q + 1) * QUARTER)
-            if q >= 2:
-                done = slice(0 if q == 2 else q * QUARTER, (q + 1) * QUARTER)
-                nc.sync.dma_start(out_words[:, done], y_codes[:, done].bitcast(I32))
+        nc.sync.dma_start(out_words, y_codes[:].bitcast(I32))
         for r in range(4):
             queue = nc.sync if r % 2 else nc.scalar
             queue.dma_start(out_2[0, r:16:4, :].bitcast(I32), y_scales[r:P:32, :].bitcast(I32))

@@ -32,7 +32,6 @@ def tile_attend_bilinearfuse_pl_kernel(
     nc = tc.nc
     with ExitStack() as ctx:
         keep = ctx.enter_context(tc.tile_pool(name="keep", bufs=1))
-        late = ctx.enter_context(tc.tile_pool(name="late", bufs=1))
         psum = ctx.enter_context(tc.psum_pool(name="psum", bufs=4))
 
         def new(shape, dtype, name, tag=None):
@@ -46,7 +45,8 @@ def tile_attend_bilinearfuse_pl_kernel(
         q_scales = new([P, TABLE], U8, "q_scales")
         i_scales = new([P, TABLE], U8, "i_scales")
         raw = {n: new([P, PACK, WIDTH], F32, n + "_raw") for n in ("wq", "wi")}
-        raw["wo"] = late.tile([P, PACK, WIDTH], F32, name="wo_raw", align_bytes=64, offset=0)
+        wo_head = new([P, PACK, PACK * WO_SPLIT], F32, "wo_head")
+        wo_tail = new([P, PACK, WIDTH - PACK * WO_SPLIT], F32, "wo_tail")
         dealt = {n: new([P, PACK * WIDTH], BF16, n + "_bf") for n in ("wq", "wi", "wo")}
         codes = {n: new([P, WIDTH], U32, n + "_codes") for n in ("wi", "wo")}
         scales = {n: new([P, WIDTH], U8, n + "_scales") for n in ("wq", "wi", "wo")}
@@ -70,9 +70,11 @@ def tile_attend_bilinearfuse_pl_kernel(
         load_words(q_words, ques_words)
         load_scales(nc.sync, i_scales, img_scales, IMG_SCALE_ROW)
         load_weight("wi", wi)
-        load_words(i_words, img_words)
         nc.sync.dma_start(gain_t[:], gain.rearrange("(p t) o -> p (t o)", t=PACK))
-        load_weight("wo", wo)
+        load_words(i_words, img_words)
+        wo_rows = wo.rearrange("(p j) c -> p j c", j=PACK)
+        nc.sync.dma_start(wo_head[:], wo_rows[:, :, : PACK * WO_SPLIT])
+        nc.sync.dma_start(wo_tail[:], wo_rows[:, :, PACK * WO_SPLIT :])
 
         def deal(copy, n, lo, hi):
             src = raw[n][:].rearrange("p j (m t) -> p m j t", t=PACK)
@@ -121,10 +123,7 @@ def tile_attend_bilinearfuse_pl_kernel(
         gained = new([P, WIDTH // 4, PACK, 4], F32, "gained")
         for t in range(PACK):
             plain = tanh_z[t // 2][:, t % 2, :].rearrange("p (c i) -> p c i", i=4)
-            if t == PACK - 1:
-                nc.vector.tensor_scalar_mul(gained[:, :, t, :], plain, gain_t[:, t : t + 1])
-            else:
-                nc.scalar.activation(gained[:, :, t, :], plain, COPY, scale=gain_t[:, t : t + 1])
+            nc.scalar.activation(gained[:, :, t, :], plain, COPY, scale=gain_t[:, t : t + 1])
 
         x_codes = new([P, WIDTH], U32, "x_codes")
         x_scales = new([P, WIDTH], U8, "x_scales")
@@ -136,13 +135,14 @@ def tile_attend_bilinearfuse_pl_kernel(
         for h in range(2):
             cols = slice(h * HALF, (h + 1) * HALF)
             nc.vector.tensor_copy(i_picked[:, cols], i_words[:].indirect(offs2_t[:, 16 * h : 16 * h + 16]))
-        deal(nc.vector.tensor_copy, "wo", 0, WO_SPLIT)
-        deal(nc.scalar.copy, "wo", WO_SPLIT, P)
+        wo_dealt = dealt["wo"][:].rearrange("p (t m j) -> p m j t", t=PACK, j=PACK)
+        nc.vector.tensor_copy(wo_dealt[:, :WO_SPLIT], wo_head[:].rearrange("p j (m t) -> p m j t", t=PACK))
+        nc.scalar.copy(wo_dealt[:, WO_SPLIT:], wo_tail[:].rearrange("p j (m t) -> p m j t", t=PACK))
 
         tanh_v_first = new([P, 32, PACK, 4], F32, "tanh_v_first")
-        tanh_v_rest = late.tile([P, 96, PACK, 4], F32, name="tanh_v_rest", align_bytes=64, offset=0)
+        tanh_v_rest = new([P, 96, PACK, 4], F32, "tanh_v_rest", "wo_tail")
         tanh_v = [tanh_v_first[:]] + [tanh_v_rest[:, 32 * q : 32 * q + 32] for q in range(3)]
-        x_first = late.tile([P, PACK * QUARTER], BF16, name="x_first", align_bytes=64, offset=6144)
+        x_first = new([P, PACK * QUARTER], BF16, "x_first", "wo_head")
         x_rest = new([P, 3 * PACK * QUARTER], BF16, "x_rest")
         x_bf = [x_first[:]] + [x_rest[:, 512 * q : 512 * q + 512] for q in range(3)]
         for q in range(4):
@@ -172,7 +172,7 @@ def tile_attend_bilinearfuse_pl_kernel(
                 product(bank[:, t, :], "wo", t, x_codes[:, cols], x_scales[:, cols])
             y_banks.append(bank)
 
-        y_bf = new([P, PACK * WIDTH], BF16, "y_bf")
+        y_bf = new([P, PACK * WIDTH], BF16, "y_bf", "x_rest")
 
         def quantise_y(lo, hi):
             nc.vector.quantize_mx(
@@ -185,13 +185,11 @@ def tile_attend_bilinearfuse_pl_kernel(
             yb = y_bf[:, PACK * q * QUARTER : PACK * (q + 1) * QUARTER]
             nc.scalar.copy(y[:], y_banks[q][:])
             nc.sync.dma_start(out_rows[:, :, cols], y[:])
-            if q == 0:
-                nc.scalar.copy(yb.rearrange("p (i t) -> p i t", t=PACK), y_banks[q][:].rearrange("p t i -> p i t"))
-            else:
-                nc.vector.tensor_copy(
-                    yb.rearrange("p (c i t) -> p c t i", i=4, t=PACK),
-                    y[:].rearrange("p t (c i) -> p c t i", i=4),
-                )
+            nc.vector.tensor_copy(
+                yb.rearrange("p (c i t) -> p c t i", i=4, t=PACK),
+                y[:].rearrange("p t (c i) -> p c t i", i=4),
+            )
+            if q > 0:
                 quantise_y(0 if q == 1 else q * QUARTER, (q + 1) * QUARTER)
         nc.sync.dma_start(out_words, y_codes[:].bitcast(I32))
         for r in range(4):

@@ -18,8 +18,7 @@ WIDTH = 512
 TABLE = 2048
 HALF = 256
 QUARTER = 128
-IMG_SCALE_ROW = 4
-WQ_SPLIT = 40
+WQ_SPLIT = 68
 WO_SPLIT = 96
 COPY = mybir.ActivationFunctionType.Copy
 
@@ -57,20 +56,33 @@ def tile_attend_bilinearfuse_pl_kernel(
         def load_words(tile, words):
             nc.sync.dma_start(tile[:].bitcast(I32), words[0].rearrange("p n t -> p (n t)").bitcast(I32))
 
-        def load_scales(queue, tile, rows, first):
+        def load_scales(tile, rows):
+            nc.scalar.dma_start(tile[0:P:8, :].bitcast(I32), rows[0].bitcast(I32))
+
+        q_rows = new([P, WIDTH], U8, "q_rows")
+        i_rows = new([P, WIDTH], U8, "i_rows")
+        q_picked_scales = new([P, WIDTH], U8, "q_picked_scales")
+        i_picked_scales = new([P, WIDTH], U8, "i_picked_scales")
+
+        def pick_scales(plane, rows, table, offsets):
+            nc.vector.tensor_copy(rows[:], table[:].indirect(offsets[:]))
             for r in range(4):
-                queue.dma_start(tile[first + r : P : 32, :].bitcast(I32), rows[0, r:16:4, :].bitcast(I32))
+                nc.sync.dma_start(plane[r:P:32, :].bitcast(I32), rows[8 * r : P : 32, :].bitcast(I32))
 
         nc.vector.memset(q_scales[:].bitcast(I32), 0)
         nc.vector.memset(i_scales[:].bitcast(I32), 0)
-        load_weight("wq", wq)
+        nc.vector.memset(q_picked_scales[:].bitcast(I32), 0)
+        nc.vector.memset(i_picked_scales[:].bitcast(I32), 0)
         nc.sync.dma_start(offs_t[:], offs)
         nc.sync.dma_start(offs2_t[:], offs2)
-        load_scales(nc.sync, q_scales, ques_scales, 0)
+        load_weight("wq", wq)
+        load_scales(q_scales, ques_scales)
+        load_scales(i_scales, img_scales)
+        nc.scalar.dma_start(gain_t[:], gain.rearrange("(p t) o -> p (t o)", t=PACK))
         load_words(q_words, ques_words)
-        load_scales(nc.sync, i_scales, img_scales, IMG_SCALE_ROW)
+        pick_scales(q_picked_scales, q_rows, q_scales, offs_t)
         load_weight("wi", wi)
-        nc.sync.dma_start(gain_t[:], gain.rearrange("(p t) o -> p (t o)", t=PACK))
+        pick_scales(i_picked_scales, i_rows, i_scales, offs2_t)
         load_words(i_words, img_words)
         wo_rows = wo.rearrange("(p j) c -> p j c", j=PACK)
         nc.sync.dma_start(wo_head[:], wo_rows[:, :, : PACK * WO_SPLIT])
@@ -97,14 +109,11 @@ def tile_attend_bilinearfuse_pl_kernel(
             )
 
         q_picked = new([P, WIDTH], U32, "q_picked")
-        q_picked_scales = new([P, WIDTH], U8, "q_picked_scales")
         i_picked = new([P, WIDTH], U32, "i_picked")
-        i_picked_scales = new([P, WIDTH], U8, "i_picked_scales")
 
         deal(nc.vector.tensor_copy, "wq", 0, WQ_SPLIT)
         deal(nc.scalar.copy, "wq", WQ_SPLIT, P)
-        nc.vector.tensor_copy(q_picked_scales[:], q_scales[:].indirect(offs_t[:]))
-        codes["wq"] = new([P, WIDTH], U32, "wq_codes", "q_scales")
+        codes["wq"] = new([P, WIDTH], U32, "wq_codes")
         quantise_weight("wq")
 
         tanh_z = [new([P, 2, WIDTH], F32, f"tanh_z{u}") for u in range(2)]
@@ -116,7 +125,6 @@ def tile_attend_bilinearfuse_pl_kernel(
                 for e in range(2):
                     product(bank[:, e, :], "wq", 2 * u + e, q_picked[:, cols], q_picked_scales[:, cols])
                 nc.scalar.activation(tanh_z[u][:, :, cols], bank[:], TANH)
-        nc.vector.tensor_copy(i_picked_scales[:], i_scales[:].indirect(offs2_t[:]))
         deal(nc.vector.tensor_copy, "wi", 0, P)
         quantise_weight("wi")
 
@@ -149,7 +157,7 @@ def tile_attend_bilinearfuse_pl_kernel(
             cols = slice(q * QUARTER, (q + 1) * QUARTER)
             bank = psum.tile([P, PACK, QUARTER], F32, name="v", bufs=2)
             for t in range(PACK):
-                product(bank[:, t, :], "wi", t, i_picked[:, cols], i_picked_scales[IMG_SCALE_ROW:P, cols])
+                product(bank[:, t, :], "wi", t, i_picked[:, cols], i_picked_scales[:, cols])
             nc.scalar.activation(
                 tanh_v[q], bank[:].rearrange("p t (c i) -> p c t i", i=4), TANH
             )

@@ -19,6 +19,8 @@ TABLE = 2048
 HALF = 256
 QUARTER = 128
 WQ_SPLIT = 68
+Q_ROWS = 112
+I_ROWS = 48
 WO_SPLIT = 96
 COPY = mybir.ActivationFunctionType.Copy
 
@@ -56,33 +58,34 @@ def tile_attend_bilinearfuse_pl_kernel(
         def load_words(tile, words):
             nc.sync.dma_start(tile[:].bitcast(I32), words[0].rearrange("p n t -> p (n t)").bitcast(I32))
 
-        def load_scales(tile, rows):
-            nc.scalar.dma_start(tile[0:P:8, :].bitcast(I32), rows[0].bitcast(I32))
+        def load_scales(tile, rows, first):
+            nc.scalar.dma_start(tile[first : first + 16, :].bitcast(I32), rows[0].bitcast(I32))
+            nc.vector.memset(tile[0:first, :].bitcast(I32), 0)
+            if first + 16 < P:
+                nc.vector.memset(tile[first + 16 : P, :].bitcast(I32), 0)
 
         q_rows = new([P, WIDTH], U8, "q_rows")
         i_rows = new([P, WIDTH], U8, "i_rows")
         q_picked_scales = new([P, WIDTH], U8, "q_picked_scales")
         i_picked_scales = new([P, WIDTH], U8, "i_picked_scales")
 
-        def pick_scales(plane, rows, table, offsets):
+        def pick_scales(plane, rows, table, offsets, first):
             nc.vector.tensor_copy(rows[:], table[:].indirect(offsets[:]))
             for r in range(4):
-                nc.sync.dma_start(plane[r:P:32, :].bitcast(I32), rows[8 * r : P : 32, :].bitcast(I32))
+                nc.sync.dma_start(plane[r:P:32, :].bitcast(I32), rows[first + r : first + 16 : 4, :].bitcast(I32))
 
-        nc.vector.memset(q_scales[:].bitcast(I32), 0)
-        nc.vector.memset(i_scales[:].bitcast(I32), 0)
+        load_scales(q_scales, ques_scales, Q_ROWS)
+        load_scales(i_scales, img_scales, I_ROWS)
         nc.vector.memset(q_picked_scales[:].bitcast(I32), 0)
         nc.vector.memset(i_picked_scales[:].bitcast(I32), 0)
         nc.sync.dma_start(offs_t[:], offs)
-        nc.sync.dma_start(offs2_t[:], offs2)
         load_weight("wq", wq)
-        load_scales(q_scales, ques_scales)
-        load_scales(i_scales, img_scales)
+        nc.sync.dma_start(offs2_t[:], offs2)
         nc.scalar.dma_start(gain_t[:], gain.rearrange("(p t) o -> p (t o)", t=PACK))
         load_words(q_words, ques_words)
-        pick_scales(q_picked_scales, q_rows, q_scales, offs_t)
+        pick_scales(q_picked_scales, q_rows, q_scales, offs_t, Q_ROWS)
         load_weight("wi", wi)
-        pick_scales(i_picked_scales, i_rows, i_scales, offs2_t)
+        pick_scales(i_picked_scales, i_rows, i_scales, offs2_t, I_ROWS)
         load_words(i_words, img_words)
         wo_rows = wo.rearrange("(p j) c -> p j c", j=PACK)
         nc.sync.dma_start(wo_head[:], wo_rows[:, :, : PACK * WO_SPLIT])

@@ -10,6 +10,7 @@ U16 = mybir.dt.uint16
 U8 = mybir.dt.uint8
 FP8X4 = mybir.dt.float8_e4m3fn_x4
 TANH = mybir.ActivationFunctionType.Tanh
+COPY = mybir.ActivationFunctionType.Copy
 MULT = mybir.AluOpType.mult
 
 P = 128
@@ -17,12 +18,11 @@ PACK = 4
 WIDTH = 512
 TABLE = 2048
 HALF = 256
-QUARTER = 128
-WQ_SPLIT = 68
 Q_ROWS = 112
 I_ROWS = 48
-WO_SPLIT = 96
-COPY = mybir.ActivationFunctionType.Copy
+WQ_VECTOR = 68
+WO_CUTS = [[0,96],[96,128]]
+PARTS = [[0,128],[128,256],[256,384],[384,512]]
 
 FLOPS = 3 * 2 * 512 * 512 * 512
 
@@ -45,15 +45,19 @@ def tile_attend_bilinearfuse_pl_kernel(
         i_words = new([P, TABLE], U32, "i_words")
         q_scales = new([P, TABLE], U8, "q_scales")
         i_scales = new([P, TABLE], U8, "i_scales")
-        raw = {n: new([P, PACK, WIDTH], F32, n + "_raw") for n in ("wq", "wi")}
-        wo_head = new([P, PACK, PACK * WO_SPLIT], F32, "wo_head")
-        wo_tail = new([P, PACK, WIDTH - PACK * WO_SPLIT], F32, "wo_tail")
+        q_rows = new([P, WIDTH], U8, "q_rows")
+        i_rows = new([P, WIDTH], U8, "i_rows")
+        q_plane = new([P, WIDTH], U8, "q_plane")
+        i_plane = new([P, WIDTH], U8, "i_plane")
+        wq_raw = new([P, PACK, WIDTH], F32, "wq_raw")
+        wi_raw = new([P, PACK, WIDTH], F32, "wi_raw")
+        wo_raw = [new([P, PACK, PACK * (hi - lo)], F32, f"wo_raw{lo}") for lo, hi in WO_CUTS]
         dealt = {n: new([P, PACK * WIDTH], BF16, n + "_bf") for n in ("wq", "wi", "wo")}
-        codes = {n: new([P, WIDTH], U32, n + "_codes") for n in ("wi", "wo")}
+        codes = {n: new([P, WIDTH], U32, n + "_codes") for n in ("wq", "wi", "wo")}
         scales = {n: new([P, WIDTH], U8, n + "_scales") for n in ("wq", "wi", "wo")}
 
-        def load_weight(n, w):
-            nc.sync.dma_start(raw[n][:], w.rearrange("(p j) c -> p j c", j=PACK))
+        def rows_of(w):
+            return w.rearrange("(p j) c -> p j c", j=PACK)
 
         def load_words(tile, words):
             nc.sync.dma_start(tile[:].bitcast(I32), words[0].rearrange("p n t -> p (n t)").bitcast(I32))
@@ -64,11 +68,6 @@ def tile_attend_bilinearfuse_pl_kernel(
             if first + 16 < P:
                 nc.vector.memset(tile[first + 16 : P, :].bitcast(I32), 0)
 
-        q_rows = new([P, WIDTH], U8, "q_rows")
-        i_rows = new([P, WIDTH], U8, "i_rows")
-        q_picked_scales = new([P, WIDTH], U8, "q_picked_scales")
-        i_picked_scales = new([P, WIDTH], U8, "i_picked_scales")
-
         def pick_scales(plane, rows, table, offsets, first):
             nc.vector.tensor_copy(rows[:], table[:].indirect(offsets[:]))
             for r in range(4):
@@ -76,25 +75,24 @@ def tile_attend_bilinearfuse_pl_kernel(
 
         load_scales(q_scales, ques_scales, Q_ROWS)
         load_scales(i_scales, img_scales, I_ROWS)
-        nc.vector.memset(q_picked_scales[:].bitcast(I32), 0)
-        nc.vector.memset(i_picked_scales[:].bitcast(I32), 0)
+        nc.vector.memset(q_plane[:].bitcast(I32), 0)
+        nc.vector.memset(i_plane[:].bitcast(I32), 0)
         nc.sync.dma_start(offs_t[:], offs)
-        load_weight("wq", wq)
+        nc.sync.dma_start(wq_raw[:], rows_of(wq))
         nc.sync.dma_start(offs2_t[:], offs2)
         nc.scalar.dma_start(gain_t[:], gain.rearrange("(p t) o -> p (t o)", t=PACK))
         load_words(q_words, ques_words)
-        pick_scales(q_picked_scales, q_rows, q_scales, offs_t, Q_ROWS)
-        load_weight("wi", wi)
-        pick_scales(i_picked_scales, i_rows, i_scales, offs2_t, I_ROWS)
+        pick_scales(q_plane, q_rows, q_scales, offs_t, Q_ROWS)
+        nc.sync.dma_start(wi_raw[:], rows_of(wi))
+        pick_scales(i_plane, i_rows, i_scales, offs2_t, I_ROWS)
         load_words(i_words, img_words)
-        wo_rows = wo.rearrange("(p j) c -> p j c", j=PACK)
-        nc.sync.dma_start(wo_head[:], wo_rows[:, :, : PACK * WO_SPLIT])
-        nc.sync.dma_start(wo_tail[:], wo_rows[:, :, PACK * WO_SPLIT :])
+        for (lo, hi), raw in zip(WO_CUTS, wo_raw):
+            nc.sync.dma_start(raw[:], rows_of(wo)[:, :, PACK * lo : PACK * hi])
 
-        def deal(copy, n, lo, hi):
-            src = raw[n][:].rearrange("p j (m t) -> p m j t", t=PACK)
+        def deal(copy, n, raw, lo, hi, at=0):
+            src = raw[:].rearrange("p j (m t) -> p m j t", t=PACK)
             dst = dealt[n][:].rearrange("p (t m j) -> p m j t", t=PACK, j=PACK)
-            copy(dst[:, lo:hi], src[:, lo:hi])
+            copy(dst[:, lo:hi], src[:, lo - at : hi - at])
 
         def quantise_weight(n):
             nc.vector.quantize_mx(codes[n][:].bitcast(FP8X4), scales[n][:], dealt[n][:])
@@ -111,13 +109,11 @@ def tile_attend_bilinearfuse_pl_kernel(
                 stop=True,
             )
 
-        q_picked = new([P, WIDTH], U32, "q_picked")
-        i_picked = new([P, WIDTH], U32, "i_picked")
-
-        deal(nc.vector.tensor_copy, "wq", 0, WQ_SPLIT)
-        deal(nc.scalar.copy, "wq", WQ_SPLIT, P)
-        codes["wq"] = new([P, WIDTH], U32, "wq_codes")
+        deal(nc.vector.tensor_copy, "wq", wq_raw, 0, WQ_VECTOR)
+        deal(nc.scalar.copy, "wq", wq_raw, WQ_VECTOR, P)
         quantise_weight("wq")
+        q_picked = new([P, WIDTH], U32, "q_picked", "wq_bf")
+        i_picked = new([P, WIDTH], U32, "i_picked")
 
         tanh_z = [new([P, 2, WIDTH], F32, f"tanh_z{u}") for u in range(2)]
         for h in range(2):
@@ -126,9 +122,9 @@ def tile_attend_bilinearfuse_pl_kernel(
             for u in range(2):
                 bank = psum.tile([P, 2, HALF], F32, name="zy")
                 for e in range(2):
-                    product(bank[:, e, :], "wq", 2 * u + e, q_picked[:, cols], q_picked_scales[:, cols])
+                    product(bank[:, e, :], "wq", 2 * u + e, q_picked[:, cols], q_plane[:, cols])
                 nc.scalar.activation(tanh_z[u][:, :, cols], bank[:], TANH)
-        deal(nc.vector.tensor_copy, "wi", 0, P)
+        deal(nc.vector.tensor_copy, "wi", wi_raw, 0, P)
         quantise_weight("wi")
 
         gained = new([P, WIDTH // 4, PACK, 4], F32, "gained")
@@ -136,73 +132,112 @@ def tile_attend_bilinearfuse_pl_kernel(
             plain = tanh_z[t // 2][:, t % 2, :].rearrange("p (c i) -> p c i", i=4)
             nc.scalar.activation(gained[:, :, t, :], plain, COPY, scale=gain_t[:, t : t + 1])
 
+        for h in range(2):
+            cols = slice(h * HALF, (h + 1) * HALF)
+            nc.vector.tensor_copy(i_picked[:, cols], i_words[:].indirect(offs2_t[:, 16 * h : 16 * h + 16]))
+        for k, (lo, hi) in enumerate(WO_CUTS):
+            deal(nc.vector.tensor_copy if k < len(WO_CUTS) - 1 else nc.scalar.copy, "wo", wo_raw[k], lo, hi, lo)
+
+        lead = 128
+        tanh_v_lead = new([P, lead // 4, PACK, 4], F32, "tanh_v_lead")
+        tanh_v_rest = new([P, (WIDTH - lead) // 4, PACK, 4], F32, "tanh_v_rest", f"wo_raw{WO_CUTS[-1][0]}")
+        x_lead = new([P, PACK * lead], BF16, "x_lead", f"wo_raw{WO_CUTS[-2][0]}")
+        x_rest = new([P, PACK * (WIDTH - lead)], BF16, "x_rest")
+
+        def tanh_v(lo, hi):
+            return tanh_v_lead[:, lo // 4 : hi // 4] if hi <= lead else tanh_v_rest[:, (lo - lead) // 4 : (hi - lead) // 4]
+
+        def x_bf(lo, hi):
+            return x_lead[:, PACK * lo : PACK * hi] if hi <= lead else x_rest[:, PACK * (lo - lead) : PACK * (hi - lead)]
+
+        def make_x(lo, hi):
+            nc.vector.tensor_tensor(
+                x_bf(lo, hi).rearrange("p (c i t) -> p c t i", i=4, t=PACK),
+                gained[:, lo // 4 : hi // 4],
+                tanh_v(lo, hi),
+                MULT,
+            )
+
+        for lo in range(0, WIDTH, P):
+            bank = psum.tile([P, PACK, P], F32, name="v", bufs=2)
+            for t in range(PACK):
+                product(bank[:, t, :], "wi", t, i_picked[:, lo : lo + P], i_plane[:, lo : lo + P])
+            step = P
+            for at in range(0, P, step):
+                nc.scalar.activation(
+                    tanh_v(lo + at, lo + at + step),
+                    bank[:, :, at : at + step].rearrange("p t (c i) -> p c t i", i=4),
+                    TANH,
+                )
+
         x_codes = new([P, WIDTH], U32, "x_codes")
         x_scales = new([P, WIDTH], U8, "x_scales")
         y_codes = new([P, WIDTH], U32, "y_codes")
         y_scales = new([P, WIDTH], U8, "y_scales")
         out_rows = out_0.rearrange("(p t) i -> p t i", t=PACK)
         out_words = out_1[0].rearrange("p n t -> p (n t)").bitcast(I32)
+        y_bf = [new([P, PACK * (hi - lo)], BF16, f"y_bf{lo}") for lo, hi in PARTS]
+        y = [new([P, PACK, hi - lo], F32, f"y{lo}") for lo, hi in PARTS]
+        banks = {}
 
-        for h in range(2):
-            cols = slice(h * HALF, (h + 1) * HALF)
-            nc.vector.tensor_copy(i_picked[:, cols], i_words[:].indirect(offs2_t[:, 16 * h : 16 * h + 16]))
-        wo_dealt = dealt["wo"][:].rearrange("p (t m j) -> p m j t", t=PACK, j=PACK)
-        nc.vector.tensor_copy(wo_dealt[:, :WO_SPLIT], wo_head[:].rearrange("p j (m t) -> p m j t", t=PACK))
-        nc.scalar.copy(wo_dealt[:, WO_SPLIT:], wo_tail[:].rearrange("p j (m t) -> p m j t", t=PACK))
+        def quantise_x(q):
+            lo, hi = PARTS[q]
+            nc.vector.quantize_mx(x_codes[:, lo:hi].bitcast(FP8X4), x_scales[:, lo:hi], x_bf(lo, hi))
 
-        tanh_v_first = new([P, 32, PACK, 4], F32, "tanh_v_first")
-        tanh_v_rest = new([P, 96, PACK, 4], F32, "tanh_v_rest", "wo_tail")
-        tanh_v = [tanh_v_first[:]] + [tanh_v_rest[:, 32 * q : 32 * q + 32] for q in range(3)]
-        x_first = new([P, PACK * QUARTER], BF16, "x_first", "wo_head")
-        x_rest = new([P, 3 * PACK * QUARTER], BF16, "x_rest")
-        x_bf = [x_first[:]] + [x_rest[:, 512 * q : 512 * q + 512] for q in range(3)]
-        for q in range(4):
-            cols = slice(q * QUARTER, (q + 1) * QUARTER)
-            bank = psum.tile([P, PACK, QUARTER], F32, name="v", bufs=2)
+        def answer(q, name, bufs):
+            lo, hi = PARTS[q]
+            banks[q, name] = psum.tile([P, PACK, hi - lo], F32, name=name, bufs=bufs)
             for t in range(PACK):
-                product(bank[:, t, :], "wi", t, i_picked[:, cols], i_picked_scales[:, cols])
-            nc.scalar.activation(
-                tanh_v[q], bank[:].rearrange("p t (c i) -> p c t i", i=4), TANH
-            )
+                product(banks[q, name][:, t, :], "wo", t, x_codes[:, lo:hi], x_scales[:, lo:hi])
 
-        y_banks = []
-        for q in range(4):
-            cols = slice(q * QUARTER, (q + 1) * QUARTER)
-            xb = x_bf[q]
-            nc.vector.tensor_tensor(
-                xb.rearrange("p (c i t) -> p c t i", i=4, t=PACK),
-                gained[:, 32 * q : 32 * q + 32],
-                tanh_v[q],
-                MULT,
-            )
-            if q == 0:
-                quantise_weight("wo")
-            nc.vector.quantize_mx(x_codes[:, cols].bitcast(FP8X4), x_scales[:, cols], xb)
-            bank = psum.tile([P, PACK, QUARTER], F32, name="zy")
-            for t in range(PACK):
-                product(bank[:, t, :], "wo", t, x_codes[:, cols], x_scales[:, cols])
-            y_banks.append(bank)
+        def store_y(q):
+            lo, hi = PARTS[q]
+            nc.scalar.copy(y[q][:], banks[q, "zy"][:])
+            nc.sync.dma_start(out_rows[:, :, lo:hi], y[q][:])
 
-        y_bf = new([P, PACK * WIDTH], BF16, "y_bf", "x_rest")
+        def round_bank(copy, q, name):
+            copy(y_bf[q][:].rearrange("p (i t) -> p i t", t=PACK), banks[q, name][:].rearrange("p t i -> p i t"))
 
-        def quantise_y(lo, hi):
-            nc.vector.quantize_mx(
-                y_codes[:, lo:hi].bitcast(FP8X4), y_scales[:, lo:hi], y_bf[:, PACK * lo : PACK * hi]
-            )
-
-        for q in range(4):
-            cols = slice(q * QUARTER, (q + 1) * QUARTER)
-            y = new([P, PACK, QUARTER], F32, f"y{q}")
-            yb = y_bf[:, PACK * q * QUARTER : PACK * (q + 1) * QUARTER]
-            nc.scalar.copy(y[:], y_banks[q][:])
-            nc.sync.dma_start(out_rows[:, :, cols], y[:])
+        def round_y(q):
             nc.vector.tensor_copy(
-                yb.rearrange("p (c i t) -> p c t i", i=4, t=PACK),
-                y[:].rearrange("p t (c i) -> p c t i", i=4),
+                y_bf[q][:].rearrange("p (c i t) -> p c t i", i=4, t=PACK),
+                y[q][:].rearrange("p t (c i) -> p c t i", i=4),
             )
-            if q > 0:
-                quantise_y(0 if q == 1 else q * QUARTER, (q + 1) * QUARTER)
-        nc.sync.dma_start(out_words, y_codes[:].bitcast(I32))
+
+        def quantise_y(q):
+            lo, hi = PARTS[q]
+            nc.vector.quantize_mx(y_codes[:, lo:hi].bitcast(FP8X4), y_scales[:, lo:hi], y_bf[q][:])
+
+        def store_codes(queue, lo, hi):
+            queue.dma_start(out_words[:, lo:hi], y_codes[:, lo:hi].bitcast(I32))
+
+        make_x(0, 128)
+        quantise_weight("wo")
+        quantise_x(0)
+        answer(0, "zy", 4)
+        make_x(128, 256)
+        make_x(256, 384)
+        quantise_x(1)
+        answer(1, "zy", 4)
+        make_x(384, 512)
+        quantise_x(2)
+        answer(2, "zy", 4)
+        quantise_x(3)
+        answer(3, "zy", 4)
+        answer(3, "twin", 1)
+        store_y(0)
+        round_bank(nc.scalar.copy, 0, "zy")
+        store_y(1)
+        round_y(1)
+        quantise_y(0)
+        store_y(2)
+        round_y(2)
+        quantise_y(1)
+        quantise_y(2)
+        store_y(3)
+        round_bank(nc.vector.tensor_copy, 3, "twin")
+        quantise_y(3)
+        store_codes(nc.sync, 0, 512)
         for r in range(4):
             queue = nc.sync if r % 2 else nc.scalar
             queue.dma_start(out_2[0, r:16:4, :].bitcast(I32), y_scales[r:P:32, :].bitcast(I32))

@@ -22,7 +22,7 @@ Q_ROWS = 112
 I_ROWS = 48
 WQ_VECTOR = 68
 WO_CUTS = [[0,96],[96,128]]
-PARTS = [[0,128],[128,256],[256,384],[384,512]]
+PARTS = [[0,128],[128,256],[256,384],[384,448],[448,512]]
 
 FLOPS = 3 * 2 * 512 * 512 * 512
 
@@ -177,7 +177,7 @@ def tile_attend_bilinearfuse_pl_kernel(
         out_rows = out_0.rearrange("(p t) i -> p t i", t=PACK)
         out_words = out_1[0].rearrange("p n t -> p (n t)").bitcast(I32)
         y_bf = [new([P, PACK * (hi - lo)], BF16, f"y_bf{lo}") for lo, hi in PARTS]
-        y = [new([P, PACK, hi - lo], F32, f"y{lo}") for lo, hi in PARTS]
+        y = [new([P, PACK, P], F32, f"y{g}") for g in range(WIDTH // P)]
         banks = {}
 
         def quantise_x(q):
@@ -190,10 +190,15 @@ def tile_attend_bilinearfuse_pl_kernel(
             for t in range(PACK):
                 product(banks[q, name][:, t, :], "wo", t, x_codes[:, lo:hi], x_scales[:, lo:hi])
 
+        def y_part(q):
+            lo, hi = PARTS[q]
+            return y[lo // P][:, :, lo % P : (hi - 1) % P + 1]
+
         def store_y(q):
             lo, hi = PARTS[q]
-            nc.scalar.copy(y[q][:], banks[q, "zy"][:])
-            nc.sync.dma_start(out_rows[:, :, lo:hi], y[q][:])
+            nc.scalar.copy(y_part(q), banks[q, "zy"][:])
+            if hi % P == 0:
+                nc.sync.dma_start(out_rows[:, :, hi - P : hi], y[lo // P][:])
 
         def round_bank(copy, q, name):
             copy(y_bf[q][:].rearrange("p (i t) -> p i t", t=PACK), banks[q, name][:].rearrange("p t i -> p i t"))
@@ -201,7 +206,7 @@ def tile_attend_bilinearfuse_pl_kernel(
         def round_y(q):
             nc.vector.tensor_copy(
                 y_bf[q][:].rearrange("p (c i t) -> p c t i", i=4, t=PACK),
-                y[q][:].rearrange("p t (c i) -> p c t i", i=4),
+                y_part(q).rearrange("p t (c i) -> p c t i", i=4),
             )
 
         def quantise_y(q):
@@ -219,12 +224,15 @@ def tile_attend_bilinearfuse_pl_kernel(
         make_x(256, 384)
         quantise_x(1)
         answer(1, "zy", 4)
-        make_x(384, 512)
+        make_x(384, 448)
         quantise_x(2)
         answer(2, "zy", 4)
+        make_x(448, 512)
         quantise_x(3)
         answer(3, "zy", 4)
-        answer(3, "twin", 1)
+        quantise_x(4)
+        answer(4, "zy", 4)
+        answer(4, "twin", 1)
         store_y(0)
         round_bank(nc.scalar.copy, 0, "zy")
         store_y(1)
@@ -233,11 +241,15 @@ def tile_attend_bilinearfuse_pl_kernel(
         store_y(2)
         round_y(2)
         quantise_y(1)
-        quantise_y(2)
+        store_codes(nc.sync, 0, 256)
         store_y(3)
-        round_bank(nc.vector.tensor_copy, 3, "twin")
+        round_y(3)
+        quantise_y(2)
+        store_y(4)
+        round_bank(nc.vector.tensor_copy, 4, "twin")
         quantise_y(3)
-        store_codes(nc.sync, 0, 512)
+        quantise_y(4)
+        store_codes(nc.sync, 256, 512)
         for r in range(4):
             queue = nc.sync if r % 2 else nc.scalar
             queue.dma_start(out_2[0, r:16:4, :].bitcast(I32), y_scales[r:P:32, :].bitcast(I32))

@@ -176,7 +176,8 @@ def tile_attend_bilinearfuse_pl_kernel(
         y_scales = new([P, WIDTH], U8, "y_scales")
         out_rows = out_0.rearrange("(p t) i -> p t i", t=PACK)
         out_words = out_1[0].rearrange("p n t -> p (n t)").bitcast(I32)
-        y_bf = [new([P, PACK * (hi - lo)], BF16, f"y_bf{lo}") for lo, hi in PARTS]
+        y_all = new([P, PACK * WIDTH], BF16, "y_all")
+        y_bf = [y_all[:, PACK * lo : PACK * hi] for lo, hi in PARTS]
         y = [new([P, PACK, P], F32, f"y{g}") for g in range(WIDTH // P)]
         banks = {}
 
@@ -201,17 +202,16 @@ def tile_attend_bilinearfuse_pl_kernel(
                 nc.sync.dma_start(out_rows[:, :, hi - P : hi], y[lo // P][:])
 
         def round_bank(copy, q, name):
-            copy(y_bf[q][:].rearrange("p (i t) -> p i t", t=PACK), banks[q, name][:].rearrange("p t i -> p i t"))
+            copy(y_bf[q].rearrange("p (i t) -> p i t", t=PACK), banks[q, name][:].rearrange("p t i -> p i t"))
 
         def round_y(q):
             nc.vector.tensor_copy(
-                y_bf[q][:].rearrange("p (c i t) -> p c t i", i=4, t=PACK),
+                y_bf[q].rearrange("p (c i t) -> p c t i", i=4, t=PACK),
                 y_part(q).rearrange("p t (c i) -> p c t i", i=4),
             )
 
-        def quantise_y(q):
-            lo, hi = PARTS[q]
-            nc.vector.quantize_mx(y_codes[:, lo:hi].bitcast(FP8X4), y_scales[:, lo:hi], y_bf[q][:])
+        def quantise_y(lo, hi):
+            nc.vector.quantize_mx(y_codes[:, lo:hi].bitcast(FP8X4), y_scales[:, lo:hi], y_all[:, PACK * lo : PACK * hi])
 
         def store_codes(queue, lo, hi):
             queue.dma_start(out_words[:, lo:hi], y_codes[:, lo:hi].bitcast(I32))
@@ -232,23 +232,20 @@ def tile_attend_bilinearfuse_pl_kernel(
         answer(3, "zy", 4)
         quantise_x(4)
         answer(4, "zy", 4)
-        answer(4, "twin", 1)
         store_y(0)
         round_bank(nc.scalar.copy, 0, "zy")
         store_y(1)
         round_y(1)
-        quantise_y(0)
         store_y(2)
         round_y(2)
-        quantise_y(1)
+        quantise_y(0, 256)
         store_codes(nc.sync, 0, 256)
         store_y(3)
         round_y(3)
-        quantise_y(2)
         store_y(4)
-        round_bank(nc.vector.tensor_copy, 4, "twin")
-        quantise_y(3)
-        quantise_y(4)
+        round_bank(nc.scalar.copy, 4, "zy")
+        quantise_y(256, 384)
+        quantise_y(384, 512)
         store_codes(nc.sync, 256, 512)
         for r in range(4):
             queue = nc.sync if r % 2 else nc.scalar

@@ -158,10 +158,16 @@ def tile_attend_bilinearfuse_pl_kernel(
                 MULT,
             )
 
+        def warm_up(n):
+            spare = psum.tile([P, WIDTH], F32, name="spare", bufs=1)
+            product(spare[:], n, 0, i_picked[:], i_plane[:])
+
         for lo in range(0, WIDTH, P):
             bank = psum.tile([P, PACK, P], F32, name="v", bufs=2)
             for t in range(PACK):
                 product(bank[:, t, :], "wi", t, i_picked[:, lo : lo + P], i_plane[:, lo : lo + P])
+            if lo == P:
+                warm_up("wi")
             step = P
             for at in range(0, P, step):
                 nc.scalar.activation(
@@ -220,6 +226,7 @@ def tile_attend_bilinearfuse_pl_kernel(
         quantise_weight("wo")
         quantise_x(0)
         answer(0, "zy", 4)
+        warm_up("wo")
         make_x(128, 256)
         make_x(256, 384)
         quantise_x(1)

@@ -84,8 +84,8 @@ def tile_attend_bilinearfuse_pl_kernel(
         load_words(q_words, ques_words)
         pick_scales(q_plane, q_rows, q_scales, offs_t, Q_ROWS)
         nc.sync.dma_start(wi_raw[:], rows_of(wi))
-        pick_scales(i_plane, i_rows, i_scales, offs2_t, I_ROWS)
         load_words(i_words, img_words)
+        pick_scales(i_plane, i_rows, i_scales, offs2_t, I_ROWS)
         for (lo, hi), raw in zip(WO_CUTS, wo_raw):
             nc.sync.dma_start(raw[:], rows_of(wo)[:, :, PACK * lo : PACK * hi])
 

@@ -22,6 +22,7 @@ Q_ROWS = 112
 I_ROWS = 48
 WQ_VECTOR = 68
 WO_CUTS = [[0,96],[96,128]]
+Z_BANKS = [[[0, 1], [1, 2], [2, 4]], [[0, 2], [2, 4]]]
 PARTS = [[0,128],[128,256],[256,384],[384,448],[448,512]]
 
 FLOPS = 3 * 2 * 512 * 512 * 512
@@ -119,11 +120,11 @@ def tile_attend_bilinearfuse_pl_kernel(
         for h in range(2):
             cols = slice(h * HALF, (h + 1) * HALF)
             nc.vector.tensor_copy(q_picked[:, cols], q_words[:].indirect(offs_t[:, 16 * h : 16 * h + 16]))
-            for u in range(2):
-                bank = psum.tile([P, 2, HALF], F32, name="zy")
-                for e in range(2):
-                    product(bank[:, e, :], "wq", 2 * u + e, q_picked[:, cols], q_plane[:, cols])
-                nc.scalar.activation(tanh_z[u][:, :, cols], bank[:], TANH)
+            for lo, hi in Z_BANKS[h]:
+                bank = psum.tile([P, hi - lo, HALF], F32, name="zy")
+                for t in range(lo, hi):
+                    product(bank[:, t - lo, :], "wq", t, q_picked[:, cols], q_plane[:, cols])
+                nc.scalar.activation(tanh_z[lo // 2][:, lo % 2 : (hi - 1) % 2 + 1, cols], bank[:], TANH)
         deal(nc.vector.tensor_copy, "wi", wi_raw, 0, P)
         quantise_weight("wi")
 
@@ -183,8 +184,7 @@ def tile_attend_bilinearfuse_pl_kernel(
         out_rows = out_0.rearrange("(p t) i -> p t i", t=PACK)
         out_words = out_1[0].rearrange("p n t -> p (n t)").bitcast(I32)
         y_all = new([P, PACK * WIDTH], BF16, "y_all")
-        y_bf = [y_all[:, PACK * lo : PACK * hi] for lo, hi in PARTS]
-        y = [new([P, PACK, P], F32, f"y{g}") for g in range(WIDTH // P)]
+        y = [new([P, PACK, HALF], F32, f"y{h}") for h in range(2)]
         banks = {}
 
         def quantise_x(q):
@@ -197,23 +197,26 @@ def tile_attend_bilinearfuse_pl_kernel(
             for t in range(PACK):
                 product(banks[q, name][:, t, :], "wo", t, x_codes[:, lo:hi], x_scales[:, lo:hi])
 
-        def y_part(q):
-            lo, hi = PARTS[q]
-            return y[lo // P][:, :, lo % P : (hi - 1) % P + 1]
+        def y_at(lo, hi):
+            return y[lo // HALF][:, :, lo % HALF : (hi - 1) % HALF + 1]
 
         def store_y(q):
             lo, hi = PARTS[q]
-            nc.scalar.copy(y_part(q), banks[q, "zy"][:])
+            nc.scalar.copy(y_at(lo, hi), banks[q, "zy"][:])
             if hi % P == 0:
-                nc.sync.dma_start(out_rows[:, :, hi - P : hi], y[lo // P][:])
+                nc.sync.dma_start(out_rows[:, :, hi - P : hi], y_at(hi - P, hi))
 
-        def round_bank(copy, q, name):
-            copy(y_bf[q].rearrange("p (i t) -> p i t", t=PACK), banks[q, name][:].rearrange("p t i -> p i t"))
+        def round_bank(q, lo, hi):
+            at = PARTS[q][0]
+            nc.scalar.copy(
+                y_all[:, PACK * lo : PACK * hi].rearrange("p (i t) -> p i t", t=PACK),
+                banks[q, "zy"][:, :, lo - at : hi - at].rearrange("p t i -> p i t"),
+            )
 
-        def round_y(q):
+        def round_y(lo, hi):
             nc.vector.tensor_copy(
-                y_bf[q].rearrange("p (c i t) -> p c t i", i=4, t=PACK),
-                y_part(q).rearrange("p t (c i) -> p c t i", i=4),
+                y_all[:, PACK * lo : PACK * hi].rearrange("p (c i t) -> p c t i", i=4, t=PACK),
+                y_at(lo, hi).rearrange("p t (c i) -> p c t i", i=4),
             )
 
         def quantise_y(lo, hi):
@@ -228,9 +231,10 @@ def tile_attend_bilinearfuse_pl_kernel(
         answer(0, "zy", 4)
         warm_up("wo")
         make_x(128, 256)
-        make_x(256, 384)
+        make_x(256, 320)
         quantise_x(1)
         answer(1, "zy", 4)
+        make_x(320, 384)
         make_x(384, 448)
         quantise_x(2)
         answer(2, "zy", 4)
@@ -240,17 +244,18 @@ def tile_attend_bilinearfuse_pl_kernel(
         quantise_x(4)
         answer(4, "zy", 4)
         store_y(0)
-        round_bank(nc.scalar.copy, 0, "zy")
+        round_bank(0, 0, 64)
         store_y(1)
-        round_y(1)
+        round_bank(1, 192, 256)
+        round_y(64, 192)
         store_y(2)
-        round_y(2)
+        round_y(256, 384)
         quantise_y(0, 256)
         store_codes(nc.sync, 0, 256)
         store_y(3)
-        round_y(3)
+        round_bank(3, 384, 448)
         store_y(4)
-        round_bank(nc.scalar.copy, 4, "zy")
+        round_bank(4, 448, 512)
         quantise_y(256, 384)
         quantise_y(384, 512)
         store_codes(nc.sync, 256, 512)

@@ -167,7 +167,7 @@ def tile_attend_bilinearfuse_pl_kernel(
             bank = psum.tile([P, PACK, P], F32, name="v", bufs=2)
             for t in range(PACK):
                 product(bank[:, t, :], "wi", t, i_picked[:, lo : lo + P], i_plane[:, lo : lo + P])
-            if lo == P:
+            if lo in (P, 2 * P):
                 warm_up("wi")
             step = P
             for at in range(0, P, step):

@@ -37,7 +37,7 @@ def tile_attend_bilinearfuse_pl_kernel(
         psum = ctx.enter_context(tc.psum_pool(name="psum", bufs=4))
 
         def new(shape, dtype, name, tag=None):
-            return keep.tile(shape, dtype, name=name, tag=tag or name, align_bytes=64)
+            return keep.tile(shape, dtype, name=name, tag=tag or name, align_bytes=256)
 
         offs_t = keep.tile([P, WIDTH // 16], U16, name="offs_t")
         offs2_t = keep.tile([P, WIDTH // 16], U16, name="offs2_t")

@@ -25,6 +25,8 @@ WO_CUTS = [[0,96],[96,128]]
 Z_BANKS = [[[0, 1], [1, 2], [2, 4]], [[0, 2], [2, 4]]]
 PARTS = [[0,128],[128,256],[256,384],[384,448],[448,512]]
 
+V_BANKS = [0, 1, 2, 1]
+
 FLOPS = 3 * 2 * 512 * 512 * 512
 
 
@@ -159,23 +161,14 @@ def tile_attend_bilinearfuse_pl_kernel(
                 MULT,
             )
 
-        def warm_up(n):
-            spare = psum.tile([P, WIDTH], F32, name="spare", bufs=1)
-            product(spare[:], n, 0, i_picked[:], i_plane[:])
-
         for lo in range(0, WIDTH, P):
-            bank = psum.tile([P, PACK, P], F32, name="v", bufs=2)
+            bank = psum.tile([P, PACK, P], F32, name=f"v{V_BANKS[lo // P]}", bufs=1)
             for t in range(PACK):
                 product(bank[:, t, :], "wi", t, i_picked[:, lo : lo + P], i_plane[:, lo : lo + P])
-            if lo in (P, 2 * P):
-                warm_up("wi")
-            step = P
-            for at in range(0, P, step):
-                nc.scalar.activation(
-                    tanh_v(lo + at, lo + at + step),
-                    bank[:, :, at : at + step].rearrange("p t (c i) -> p c t i", i=4),
-                    TANH,
-                )
+            if lo == 2 * P:
+                spare = psum.tile([P, WIDTH], F32, name="v0", bufs=1)
+                product(spare[:], "wi", 0, codes["wi"][:], scales["wi"][:])
+            nc.scalar.activation(tanh_v(lo, lo + P), bank[:].rearrange("p t (c i) -> p c t i", i=4), TANH)
 
         x_codes = new([P, WIDTH], U32, "x_codes")
         x_scales = new([P, WIDTH], U8, "x_scales")
@@ -229,7 +222,6 @@ def tile_attend_bilinearfuse_pl_kernel(
         quantise_weight("wo")
         quantise_x(0)
         answer(0, "zy", 4)
-        warm_up("wo")
         make_x(128, 256)
         make_x(256, 320)
         quantise_x(1)

@@ -234,6 +234,7 @@ def tile_attend_bilinearfuse_pl_kernel(
         quantise_x(3)
         answer(3, "zy", 4)
         quantise_x(4)
+        answer(4, "v2", 1)
         answer(4, "zy", 4)
         store_y(0)
         round_bank(0, 0, 64)
@@ -247,7 +248,9 @@ def tile_attend_bilinearfuse_pl_kernel(
         store_y(3)
         round_bank(3, 384, 448)
         store_y(4)
-        round_bank(4, 448, 512)
+        nc.vector.tensor_copy(
+            y_all[:, PACK * 448 :].rearrange("p (i t) -> p i t", t=PACK), banks[4, "v2"][:].rearrange("p t i -> p i t")
+        )
         quantise_y(256, 384)
         quantise_y(384, 512)
         store_codes(nc.sync, 256, 512)

@@ -253,7 +253,7 @@ def tile_attend_bilinearfuse_pl_kernel(
         )
         quantise_y(256, 384)
         quantise_y(384, 512)
-        store_codes(nc.sync, 256, 512)
         for r in range(4):
             queue = nc.sync if r % 2 else nc.scalar
             queue.dma_start(out_2[0, r:16:4, :].bitcast(I32), y_scales[r:P:32, :].bitcast(I32))
+        store_codes(nc.sync, 256, 512)

@@ -18,14 +18,14 @@ PACK = 4
 WIDTH = 512
 TABLE = 2048
 HALF = 256
-Q_ROWS = 112
-I_ROWS = 48
+ROWS = 112
 WQ_VECTOR = 68
 WO_CUTS = [[0,96],[96,128]]
-Z_BANKS = [[[0, 1], [1, 2], [2, 4]], [[0, 2], [2, 4]]]
+Z_PLACES = [[[0, 2], [2, 4]], [[0, 4]], [[0, 2], [2, 4]]]
 PARTS = [[0,128],[128,256],[256,384],[384,448],[448,512]]
 
 V_BANKS = [0, 1, 2, 1]
+I_GATHERS = [[0, 128], [128, 256], [256, 512]]
 
 FLOPS = 3 * 2 * 512 * 512 * 512
 
@@ -48,13 +48,15 @@ def tile_attend_bilinearfuse_pl_kernel(
         i_words = new([P, TABLE], U32, "i_words")
         q_scales = new([P, TABLE], U8, "q_scales")
         i_scales = new([P, TABLE], U8, "i_scales")
-        q_rows = new([P, WIDTH], U8, "q_rows")
-        i_rows = new([P, WIDTH], U8, "i_rows")
-        q_plane = new([P, WIDTH], U8, "q_plane")
-        i_plane = new([P, WIDTH], U8, "i_plane")
+        rows = new([P, 2 * WIDTH], U8, "rows")
+        planes = new([P, 2 * WIDTH], U8, "planes")
+        q_plane = planes[:, :WIDTH]
+        i_plane = planes[:, WIDTH:]
         wq_raw = new([P, PACK, WIDTH], F32, "wq_raw")
         wi_raw = new([P, PACK, WIDTH], F32, "wi_raw")
-        wo_raw = [new([P, PACK, PACK * (hi - lo)], F32, f"wo_raw{lo}") for lo, hi in WO_CUTS]
+        wo_first = new([P, PACK * 384], F32, "wo_first")
+        wo_last = new([P, 448 + WIDTH], F32, "wo_last")
+        wo_raw = [t.rearrange("p (j c) -> p j c", j=PACK) for t in (wo_first[:], wo_last[:, :WIDTH])]
         dealt = {n: new([P, PACK * WIDTH], BF16, n + "_bf") for n in ("wq", "wi", "wo")}
         codes = {n: new([P, WIDTH], U32, n + "_codes") for n in ("wq", "wi", "wo")}
         scales = {n: new([P, WIDTH], U8, n + "_scales") for n in ("wq", "wi", "wo")}
@@ -65,30 +67,29 @@ def tile_attend_bilinearfuse_pl_kernel(
         def load_words(tile, words):
             nc.sync.dma_start(tile[:].bitcast(I32), words[0].rearrange("p n t -> p (n t)").bitcast(I32))
 
-        def load_scales(tile, rows, first):
-            nc.scalar.dma_start(tile[first : first + 16, :].bitcast(I32), rows[0].bitcast(I32))
-            nc.vector.memset(tile[0:first, :].bitcast(I32), 0)
-            if first + 16 < P:
-                nc.vector.memset(tile[first + 16 : P, :].bitcast(I32), 0)
+        def load_scales(tile, table):
+            nc.scalar.dma_start(tile[ROWS:P, :].bitcast(I32), table[0].bitcast(I32))
+            nc.vector.memset(tile[0:ROWS, :].bitcast(I32), 0)
 
-        def pick_scales(plane, rows, table, offsets, first):
-            nc.vector.tensor_copy(rows[:], table[:].indirect(offsets[:]))
+        def move_scales(lo, hi):
             for r in range(4):
-                nc.sync.dma_start(plane[r:P:32, :].bitcast(I32), rows[first + r : first + 16 : 4, :].bitcast(I32))
+                nc.sync.dma_start(planes[r:P:32, lo:hi].bitcast(I32), rows[ROWS + r : P : 4, lo:hi].bitcast(I32))
 
-        load_scales(q_scales, ques_scales, Q_ROWS)
-        load_scales(i_scales, img_scales, I_ROWS)
-        nc.vector.memset(q_plane[:].bitcast(I32), 0)
-        nc.vector.memset(i_plane[:].bitcast(I32), 0)
+        load_scales(q_scales, ques_scales)
+        load_scales(i_scales, img_scales)
+        nc.vector.memset(planes[:].bitcast(I32), 0)
         nc.sync.dma_start(offs_t[:], offs)
-        nc.sync.dma_start(wq_raw[:], rows_of(wq))
         nc.sync.dma_start(offs2_t[:], offs2)
+        nc.sync.dma_start(wq_raw[:], rows_of(wq))
         nc.scalar.dma_start(gain_t[:], gain.rearrange("(p t) o -> p (t o)", t=PACK))
         load_words(q_words, ques_words)
-        pick_scales(q_plane, q_rows, q_scales, offs_t, Q_ROWS)
+        nc.vector.tensor_copy(rows[:, :WIDTH], q_scales[:].indirect(offs_t[:]))
+        nc.vector.tensor_copy(rows[:, WIDTH : WIDTH + HALF], i_scales[:].indirect(offs2_t[:, :16]))
+        move_scales(0, WIDTH + HALF)
+        nc.vector.tensor_copy(rows[:, WIDTH + HALF :], i_scales[:].indirect(offs2_t[:, 16:]))
         nc.sync.dma_start(wi_raw[:], rows_of(wi))
         load_words(i_words, img_words)
-        pick_scales(i_plane, i_rows, i_scales, offs2_t, I_ROWS)
+        move_scales(WIDTH + HALF, 2 * WIDTH)
         for (lo, hi), raw in zip(WO_CUTS, wo_raw):
             nc.sync.dma_start(raw[:], rows_of(wo)[:, :, PACK * lo : PACK * hi])
 
@@ -118,37 +119,42 @@ def tile_attend_bilinearfuse_pl_kernel(
         q_picked = new([P, WIDTH], U32, "q_picked", "wq_bf")
         i_picked = new([P, WIDTH], U32, "i_picked")
 
-        tanh_z = [new([P, 2, WIDTH], F32, f"tanh_z{u}") for u in range(2)]
-        for h in range(2):
-            cols = slice(h * HALF, (h + 1) * HALF)
-            nc.vector.tensor_copy(q_picked[:, cols], q_words[:].indirect(offs_t[:, 16 * h : 16 * h + 16]))
-            for lo, hi in Z_BANKS[h]:
-                bank = psum.tile([P, hi - lo, HALF], F32, name="zy")
+        tanh_z = new([P, PACK, WIDTH], F32, "tanh_z")
+        for (a, b), places in zip(I_GATHERS, Z_PLACES):
+            nc.vector.tensor_copy(q_picked[:, a:b], q_words[:].indirect(offs_t[:, a // 16 : b // 16]))
+            for lo, hi in places:
+                bank = psum.tile([P, hi - lo, b - a], F32, name="zy")
                 for t in range(lo, hi):
-                    product(bank[:, t - lo, :], "wq", t, q_picked[:, cols], q_plane[:, cols])
-                nc.scalar.activation(tanh_z[lo // 2][:, lo % 2 : (hi - 1) % 2 + 1, cols], bank[:], TANH)
+                    product(bank[:, t - lo, :], "wq", t, q_picked[:, a:b], q_plane[:, a:b])
+                nc.scalar.activation(tanh_z[:, lo:hi, a:b], bank[:], TANH)
         deal(nc.vector.tensor_copy, "wi", wi_raw, 0, P)
         quantise_weight("wi")
 
         gained = new([P, WIDTH // 4, PACK, 4], F32, "gained")
         for t in range(PACK):
-            plain = tanh_z[t // 2][:, t % 2, :].rearrange("p (c i) -> p c i", i=4)
+            plain = tanh_z[:, t, :].rearrange("p (c i) -> p c i", i=4)
             nc.scalar.activation(gained[:, :, t, :], plain, COPY, scale=gain_t[:, t : t + 1])
 
-        for h in range(2):
-            cols = slice(h * HALF, (h + 1) * HALF)
-            nc.vector.tensor_copy(i_picked[:, cols], i_words[:].indirect(offs2_t[:, 16 * h : 16 * h + 16]))
-        for k, (lo, hi) in enumerate(WO_CUTS):
-            deal(nc.vector.tensor_copy if k < len(WO_CUTS) - 1 else nc.scalar.copy, "wo", wo_raw[k], lo, hi, lo)
+        for lo, hi in I_GATHERS:
+            nc.vector.tensor_copy(i_picked[:, lo:hi], i_words[:].indirect(offs2_t[:, lo // 16 : hi // 16]))
+        deal(nc.vector.tensor_copy, "wo", wo_raw[0], 0, 64)
+        deal(nc.vector.tensor_copy, "wo", wo_raw[0], 64, 96)
+        deal(nc.scalar.copy, "wo", wo_raw[1], 112, 128, 96)
+        deal(nc.scalar.copy, "wo", wo_raw[1], 96, 112, 96)
 
         lead = 128
-        tanh_v_lead = new([P, lead // 4, PACK, 4], F32, "tanh_v_lead")
-        tanh_v_rest = new([P, (WIDTH - lead) // 4, PACK, 4], F32, "tanh_v_rest", f"wo_raw{WO_CUTS[-1][0]}")
-        x_lead = new([P, PACK * lead], BF16, "x_lead", f"wo_raw{WO_CUTS[-2][0]}")
+        tanh_v_parts = [
+            new([P, WIDTH], F32, "tanh_v0")[:],
+            wo_last[:, 448:],
+            wo_first[:, 384 : 384 + WIDTH],
+            new([P, WIDTH], F32, "tanh_v3")[:],
+        ]
+        x_lead = wo_first[:, :HALF].bitcast(BF16)
         x_rest = new([P, PACK * (WIDTH - lead)], BF16, "x_rest")
 
         def tanh_v(lo, hi):
-            return tanh_v_lead[:, lo // 4 : hi // 4] if hi <= lead else tanh_v_rest[:, (lo - lead) // 4 : (hi - lead) // 4]
+            part = tanh_v_parts[lo // P].rearrange("p (c t i) -> p c t i", t=PACK, i=4)
+            return part[:, lo % P // 4 : ((hi - 1) % P + 1) // 4]
 
         def x_bf(lo, hi):
             return x_lead[:, PACK * lo : PACK * hi] if hi <= lead else x_rest[:, PACK * (lo - lead) : PACK * (hi - lead)]

from contextlib import ExitStack

import concourse.mybir as mybir

F32 = mybir.dt.float32
BF16 = mybir.dt.bfloat16
I32 = mybir.dt.int32
U32 = mybir.dt.uint32
U16 = mybir.dt.uint16
U8 = mybir.dt.uint8
FP8X4 = mybir.dt.float8_e4m3fn_x4
TANH = mybir.ActivationFunctionType.Tanh
COPY = mybir.ActivationFunctionType.Copy
MULT = mybir.AluOpType.mult

P = 128
PACK = 4
WIDTH = 512
TABLE = 2048
HALF = 256
ROWS = 112
WQ_VECTOR = 68
WO_CUTS = [[0,96],[96,128]]
Z_PLACES = [[[0, 2], [2, 4]], [[0, 4]], [[0, 2], [2, 4]]]
PARTS = [[0,128],[128,256],[256,384],[384,448],[448,512]]

V_BANKS = [0, 1, 2, 1]
I_GATHERS = [[0, 128], [128, 256], [256, 512]]

FLOPS = 3 * 2 * 512 * 512 * 512


def tile_attend_bilinearfuse_pl_kernel(
    tc, ques_words, ques_scales, img_words, img_scales, wq, wi, gain, wo, offs, offs2, out_0, out_1, out_2
):
    nc = tc.nc
    with ExitStack() as ctx:
        keep = ctx.enter_context(tc.tile_pool(name="keep", bufs=1))
        psum = ctx.enter_context(tc.psum_pool(name="psum", bufs=4))

        def new(shape, dtype, name, tag=None):
            return keep.tile(shape, dtype, name=name, tag=tag or name, align_bytes=256)

        offs_t = keep.tile([P, WIDTH // 16], U16, name="offs_t")
        offs2_t = keep.tile([P, WIDTH // 16], U16, name="offs2_t")
        gain_t = new([P, PACK], F32, "gain_t")
        q_words = new([P, TABLE], U32, "q_words")
        i_words = new([P, TABLE], U32, "i_words")
        q_scales = new([P, TABLE], U8, "q_scales")
        i_scales = new([P, TABLE], U8, "i_scales")
        rows = new([P, 2 * WIDTH], U8, "rows")
        planes = new([P, 2 * WIDTH], U8, "planes")
        q_plane = planes[:, :WIDTH]
        i_plane = planes[:, WIDTH:]
        wq_raw = new([P, PACK, WIDTH], F32, "wq_raw")
        wi_raw = new([P, PACK, WIDTH], F32, "wi_raw")
        wo_first = new([P, PACK * 384], F32, "wo_first")
        wo_last = new([P, 448 + WIDTH], F32, "wo_last")
        wo_raw = [t.rearrange("p (j c) -> p j c", j=PACK) for t in (wo_first[:], wo_last[:, :WIDTH])]
        dealt = {n: new([P, PACK * WIDTH], BF16, n + "_bf") for n in ("wq", "wi", "wo")}
        codes = {n: new([P, WIDTH], U32, n + "_codes") for n in ("wq", "wi", "wo")}
        scales = {n: new([P, WIDTH], U8, n + "_scales") for n in ("wq", "wi", "wo")}

        def rows_of(w):
            return w.rearrange("(p j) c -> p j c", j=PACK)

        def load_words(tile, words):
            nc.sync.dma_start(tile[:].bitcast(I32), words[0].rearrange("p n t -> p (n t)").bitcast(I32))

        def load_scales(tile, table):
            nc.scalar.dma_start(tile[ROWS:P, :].bitcast(I32), table[0].bitcast(I32))
            nc.vector.memset(tile[0:ROWS, :].bitcast(I32), 0)

        def move_scales(lo, hi):
            for r in range(4):
                nc.sync.dma_start(planes[r:P:32, lo:hi].bitcast(I32), rows[ROWS + r : P : 4, lo:hi].bitcast(I32))

        load_scales(q_scales, ques_scales)
        load_scales(i_scales, img_scales)
        nc.vector.memset(planes[:].bitcast(I32), 0)
        nc.sync.dma_start(offs_t[:], offs)
        nc.sync.dma_start(offs2_t[:], offs2)
        nc.sync.dma_start(wq_raw[:], rows_of(wq))
        nc.scalar.dma_start(gain_t[:], gain.rearrange("(p t) o -> p (t o)", t=PACK))
        load_words(q_words, ques_words)
        nc.vector.tensor_copy(rows[:, :WIDTH], q_scales[:].indirect(offs_t[:]))
        nc.vector.tensor_copy(rows[:, WIDTH : WIDTH + HALF], i_scales[:].indirect(offs2_t[:, :16]))
        move_scales(0, WIDTH + HALF)
        nc.vector.tensor_copy(rows[:, WIDTH + HALF :], i_scales[:].indirect(offs2_t[:, 16:]))
        nc.sync.dma_start(wi_raw[:], rows_of(wi))
        load_words(i_words, img_words)
        move_scales(WIDTH + HALF, 2 * WIDTH)
        for (lo, hi), raw in zip(WO_CUTS, wo_raw):
            nc.sync.dma_start(raw[:], rows_of(wo)[:, :, PACK * lo : PACK * hi])

        def deal(copy, n, raw, lo, hi, at=0):
            src = raw[:].rearrange("p j (m t) -> p m j t", t=PACK)
            dst = dealt[n][:].rearrange("p (t m j) -> p m j t", t=PACK, j=PACK)
            copy(dst[:, lo:hi], src[:, lo - at : hi - at])

        def quantise_weight(n):
            nc.vector.quantize_mx(codes[n][:].bitcast(FP8X4), scales[n][:], dealt[n][:])

        def product(out, n, t, rhs, rhs_scale):
            cols = slice(t * P, (t + 1) * P)
            nc.tensor.matmul_mx(
                out,
                lhsT=codes[n][:, cols].bitcast(FP8X4),
                lhsT_scale=scales[n][:, cols],
                rhs=rhs.bitcast(FP8X4),
                rhs_scale=rhs_scale,
                start=True,
                stop=True,
            )

        deal(nc.vector.tensor_copy, "wq", wq_raw, 0, WQ_VECTOR)
        deal(nc.scalar.copy, "wq", wq_raw, WQ_VECTOR, P)
        quantise_weight("wq")
        q_picked = new([P, WIDTH], U32, "q_picked", "wq_bf")
        i_picked = new([P, WIDTH], U32, "i_picked")

        tanh_z = new([P, PACK, WIDTH], F32, "tanh_z")
        for (a, b), places in zip(I_GATHERS, Z_PLACES):
            nc.vector.tensor_copy(q_picked[:, a:b], q_words[:].indirect(offs_t[:, a // 16 : b // 16]))
            for lo, hi in places:
                bank = psum.tile([P, hi - lo, b - a], F32, name="zy")
                for t in range(lo, hi):
                    product(bank[:, t - lo, :], "wq", t, q_picked[:, a:b], q_plane[:, a:b])
                nc.scalar.activation(tanh_z[:, lo:hi, a:b], bank[:], TANH)
        deal(nc.vector.tensor_copy, "wi", wi_raw, 0, P)
        quantise_weight("wi")

        gained = new([P, WIDTH // 4, PACK, 4], F32, "gained")
        for t in range(PACK):
            plain = tanh_z[:, t, :].rearrange("p (c i) -> p c i", i=4)
            nc.scalar.activation(gained[:, :, t, :], plain, COPY, scale=gain_t[:, t : t + 1])

        for lo, hi in I_GATHERS:
            nc.vector.tensor_copy(i_picked[:, lo:hi], i_words[:].indirect(offs2_t[:, lo // 16 : hi // 16]))
        deal(nc.vector.tensor_copy, "wo", wo_raw[0], 0, 64)
        deal(nc.vector.tensor_copy, "wo", wo_raw[0], 64, 96)
        deal(nc.scalar.copy, "wo", wo_raw[1], 112, 128, 96)
        deal(nc.scalar.copy, "wo", wo_raw[1], 96, 112, 96)

        lead = 128
        tanh_v_parts = [
            new([P, WIDTH], F32, "tanh_v0")[:],
            wo_last[:, 448:],
            wo_first[:, 384 : 384 + WIDTH],
            new([P, WIDTH], F32, "tanh_v3")[:],
        ]
        x_lead = wo_first[:, :HALF].bitcast(BF16)
        x_rest = new([P, PACK * (WIDTH - lead)], BF16, "x_rest")

        def tanh_v(lo, hi):
            part = tanh_v_parts[lo // P].rearrange("p (c t i) -> p c t i", t=PACK, i=4)
            return part[:, lo % P // 4 : ((hi - 1) % P + 1) // 4]

        def x_bf(lo, hi):
            return x_lead[:, PACK * lo : PACK * hi] if hi <= lead else x_rest[:, PACK * (lo - lead) : PACK * (hi - lead)]

        def make_x(lo, hi):
            nc.vector.tensor_tensor(
                x_bf(lo, hi).rearrange("p (c i t) -> p c t i", i=4, t=PACK),
                gained[:, lo // 4 : hi // 4],
                tanh_v(lo, hi),
                MULT,
            )

        for lo in range(0, WIDTH, P):
            bank = psum.tile([P, PACK, P], F32, name=f"v{V_BANKS[lo // P]}", bufs=1)
            for t in range(PACK):
                product(bank[:, t, :], "wi", t, i_picked[:, lo : lo + P], i_plane[:, lo : lo + P])
            if lo == 2 * P:
                spare = psum.tile([P, WIDTH], F32, name="v0", bufs=1)
                product(spare[:], "wi", 0, codes["wi"][:], scales["wi"][:])
            nc.scalar.activation(tanh_v(lo, lo + P), bank[:].rearrange("p t (c i) -> p c t i", i=4), TANH)

        x_codes = new([P, WIDTH], U32, "x_codes")
        x_scales = new([P, WIDTH], U8, "x_scales")
        y_codes = new([P, WIDTH], U32, "y_codes")
        y_scales = new([P, WIDTH], U8, "y_scales")
        out_rows = out_0.rearrange("(p t) i -> p t i", t=PACK)
        out_words = out_1[0].rearrange("p n t -> p (n t)").bitcast(I32)
        y_all = new([P, PACK * WIDTH], BF16, "y_all")
        y = [new([P, PACK, HALF], F32, f"y{h}") for h in range(2)]
        banks = {}

        def quantise_x(q):
            lo, hi = PARTS[q]
            nc.vector.quantize_mx(x_codes[:, lo:hi].bitcast(FP8X4), x_scales[:, lo:hi], x_bf(lo, hi))

        def answer(q, name, bufs):
            lo, hi = PARTS[q]
            banks[q, name] = psum.tile([P, PACK, hi - lo], F32, name=name, bufs=bufs)
            for t in range(PACK):
                product(banks[q, name][:, t, :], "wo", t, x_codes[:, lo:hi], x_scales[:, lo:hi])

        def y_at(lo, hi):
            return y[lo // HALF][:, :, lo % HALF : (hi - 1) % HALF + 1]

        def store_y(q):
            lo, hi = PARTS[q]
            nc.scalar.copy(y_at(lo, hi), banks[q, "zy"][:])
            if hi % P == 0:
                nc.sync.dma_start(out_rows[:, :, hi - P : hi], y_at(hi - P, hi))

        def round_bank(q, lo, hi):
            at = PARTS[q][0]
            nc.scalar.copy(
                y_all[:, PACK * lo : PACK * hi].rearrange("p (i t) -> p i t", t=PACK),
                banks[q, "zy"][:, :, lo - at : hi - at].rearrange("p t i -> p i t"),
            )

        def round_y(lo, hi):
            nc.vector.tensor_copy(
                y_all[:, PACK * lo : PACK * hi].rearrange("p (c i t) -> p c t i", i=4, t=PACK),
                y_at(lo, hi).rearrange("p t (c i) -> p c t i", i=4),
            )

        def quantise_y(lo, hi):
            nc.vector.quantize_mx(y_codes[:, lo:hi].bitcast(FP8X4), y_scales[:, lo:hi], y_all[:, PACK * lo : PACK * hi])

        def store_codes(queue, lo, hi):
            queue.dma_start(out_words[:, lo:hi], y_codes[:, lo:hi].bitcast(I32))

        make_x(0, 128)
        quantise_weight("wo")
        quantise_x(0)
        answer(0, "zy", 4)
        make_x(128, 256)
        make_x(256, 320)
        quantise_x(1)
        answer(1, "zy", 4)
        make_x(320, 384)
        make_x(384, 448)
        quantise_x(2)
        answer(2, "zy", 4)
        make_x(448, 512)
        quantise_x(3)
        answer(3, "zy", 4)
        quantise_x(4)
        answer(4, "v2", 1)
        answer(4, "zy", 4)
        store_y(0)
        round_bank(0, 0, 64)
        store_y(1)
        round_bank(1, 192, 256)
        round_y(64, 192)
        store_y(2)
        round_y(256, 384)
        quantise_y(0, 256)
        store_codes(nc.sync, 0, 256)
        store_y(3)
        round_bank(3, 384, 448)
        store_y(4)
        nc.vector.tensor_copy(
            y_all[:, PACK * 448 :].rearrange("p (i t) -> p i t", t=PACK), banks[4, "v2"][:].rearrange("p t i -> p i t")
        )
        quantise_y(256, 384)
        quantise_y(384, 512)
        for r in range(4):
            queue = nc.sync if r % 2 else nc.scalar
            queue.dma_start(out_2[0, r:16:4, :].bitcast(I32), y_scales[r:P:32, :].bitcast(I32))
        store_codes(nc.sync, 256, 512)
